import numpy as np
import ml_dtypes


def mxq(x, axis, fmt="e4m3"):
    dtype, down = {"e4m3": (ml_dtypes.float8_e4m3fn, 7), "e5m2": (ml_dtypes.float8_e5m2, 14)}[fmt]
    v = np.moveaxis(np.asarray(x, np.float32).astype(ml_dtypes.bfloat16).astype(np.float64), axis, -1)
    blocks = v.reshape(v.shape[:-1] + (-1, 32))
    amax = np.abs(blocks).max(-1, keepdims=True)
    byte = np.maximum(np.where(amax > 0, np.frexp(amax)[1] - 1 + 127, 0) - down, 1)
    scale = np.exp2(byte - 127.0)
    codes = (blocks / scale).astype(np.float32).astype(dtype).astype(np.float64)
    return np.moveaxis((codes * scale).reshape(v.shape), -1, axis)


WIDE = False


def mx_kscale(k):
    if not WIDE:
        return np.ones(k)
    levels = np.array([10, -10, 5, -5, 0])
    if k % 512:
        return np.exp2(np.random.permutation(np.resize(levels, k // 32))).repeat(32)
    a = np.empty((k // 512, 16))
    for p in range(k // 512):
        a[p, :8] = np.random.permutation(np.resize(levels, 8))
        for g in range(8):
            far = levels[np.abs(levels - a[p, g]) >= 10]
            a[p, g + 8] = far[np.random.randint(len(far))]
    return np.exp2(a.ravel()).repeat(32)


def f64(x):
    return np.asarray(x).astype(np.float64)


def striped(idx):
    return np.tile(idx.reshape(-1, 16).T, (8, 1)).astype(np.uint16)


def unstriped(offs):
    return offs[:16].T.reshape(-1).astype(np.int64)


def pack_weight(w):
    k, n = w.shape
    w = f64(np.asarray(w, np.float32).astype(ml_dtypes.bfloat16)).reshape(k // 32, 32, n)
    amax = np.abs(w).max(1)
    byte = np.clip(np.where(amax > 0, np.frexp(amax)[1] - 1 + 127 - 7, 1), 1, 254)
    scaled = (w * np.exp2(127.0 - byte)[:, None, :]).reshape(k, n).astype(np.float32)
    words = np.ascontiguousarray(scaled.reshape(k // 512, 128, 4, n).transpose(0, 1, 3, 2)).astype(ml_dtypes.float8_e4m3fn).view(np.uint8)
    return words, np.ascontiguousarray(byte.astype(np.uint8).reshape(k // 512, 16, n))


def unpack_weight(words, scales):
    g, p, n, _ = words.shape
    vals = np.ascontiguousarray(words).view(ml_dtypes.float8_e4m3fn).astype(np.float64) * np.repeat(np.exp2(scales.astype(np.float64) - 127.0), 8, axis=1)[..., None]
    return vals.transpose(0, 1, 3, 2).reshape(g * 512, n)


def sigmoid(v):
    return 1.0 / (1.0 + np.exp(-np.maximum(v, -700.0)))


K, T, S, N, U = 512, 2048, 1024, 256, 1024


def setup_inputs():
    n = np.random.standard_normal
    s = mx_kscale(K)[:, None]
    packed_w1 = pack_weight(n((K, N)) / np.sqrt(K) / s)
    packed_w2 = pack_weight(n((K, N)) / np.sqrt(K) / s)
    packed_w3 = pack_weight(n((K, N)) / np.sqrt(K) / s)
    return {
        "xT": (n((K, T)) * s).astype(np.float32),
        "w1_words": packed_w1[0],
        "w1_scales": packed_w1[1],
        "w2_words": packed_w2[0],
        "w2_scales": packed_w2[1],
        "w3_words": packed_w3[0],
        "w3_scales": packed_w3[1],
        "offs": striped(np.random.permutation(T)[:S]),
        "src": striped(np.random.permutation(S)[(S * np.random.uniform(0, 1, U) ** 4).astype(np.int64)]),
        "dst": striped(np.random.permutation(S)),
    }


def reference(xT, w1_words, w1_scales, w2_words, w2_scales, w3_words, w3_scales, offs, src, dst):
    xq = mxq(f64(xT)[:, unstriped(offs)], 0, "e4m3")
    y = unpack_weight(w1_words, w1_scales).T @ xq
    e = unpack_weight(w2_words, w2_scales).T @ xq
    h = unpack_weight(w3_words, w3_scales).T @ xq
    return (sigmoid(y[:, unstriped(dst)] + e[:, unstriped(src)])) * h[:, unstriped(src)]

@@ -1,0 +1,134 @@
+from contextlib import ExitStack
+
+import concourse.mybir as mybir
+
+K, T, S, N, U = 512, 2048, 1024, 256, 1024
+FLOPS = 3 * 2 * K * N * S
+
+F32 = mybir.dt.float32
+BF16 = mybir.dt.bfloat16
+I32 = mybir.dt.int32
+U32 = mybir.dt.uint32
+U16 = mybir.dt.uint16
+U8 = mybir.dt.uint8
+FP8X4 = mybir.dt.float8_e4m3fn_x4
+ADD = mybir.AluOpType.add
+MULT = mybir.AluOpType.mult
+COPY = mybir.ActivationFunctionType.Copy
+SIGMOID = mybir.ActivationFunctionType.Sigmoid
+
+P = 128
+PACK = 4
+HALF = S // 2
+QUANT = 256
+BANK = 512
+LOAD_CUTS = ((0, 1024, 1536, 2048), (0, 1024, 2048), (0, 1024, 2048), (0, 1024, 1792, 2048))
+VECTOR_SHARE = (256, 256, 512, 512)
+
+
+def entries(lst, a, b):
+    return lst[:, a // 16 : b // 16]
+
+
+def tile_picked_edgeatt_sigmoid_e_kernel(
+    tc, xT, w1_words, w1_scales, w2_words, w2_scales, w3_words, w3_scales, offs, src, dst, out
+):
+    nc = tc.nc
+    with ExitStack() as ctx:
+        keep = ctx.enter_context(tc.tile_pool(name="keep", bufs=1))
+        psum = ctx.enter_context(tc.psum_pool(name="psum", bufs=1))
+
+        offs_t = keep.tile([P, S // 16], U16, name="offs_t")
+        src_t = keep.tile([P, U // 16], U16, name="src_t")
+        dst_t = keep.tile([P, U // 16], U16, name="dst_t")
+        x32 = [keep.tile([P, T], F32, name="x32_%d" % j) for j in range(PACK)]
+        x16 = [keep.tile([P, T], BF16, name="x16_%d" % j) for j in range(PACK)]
+        woven = [keep.tile([P, HALF, PACK], BF16, name="woven_%d" % h, align_bytes=64) for h in range(2)]
+        x_codes = keep.tile([P, S], U32, name="x_codes", align_bytes=64)
+        x_scales = keep.tile([P, S], U8, name="x_scales", align_bytes=64)
+        w_codes = [keep.tile([P, N], I32, name="w_codes_%d" % i, align_bytes=64) for i in range(3)]
+        w_scales = [keep.tile([P, N], U8, name="w_scales_%d" % i, align_bytes=64) for i in range(3)]
+        words_in = (w1_words, w2_words, w3_words)
+        scales_in = (w1_scales, w2_scales, w3_scales)
+
+        for i in range(3):
+            nc.vector.memset(w_scales[i][:].bitcast(I32), 0)
+        warm = keep.tile([P, 2], F32, name="warm")
+        nc.vector.memset(warm[:, 0:1], 0.0)
+        nc.scalar.activation(warm[:, 1:2], warm[:, 0:1], SIGMOID)
+
+        def load_scales(queue, i):
+            rows = scales_in[i][0].bitcast(I32)
+            for q in range(4):
+                queue.dma_start(out=w_scales[i][32 * q : 32 * q + 4, :].bitcast(I32), in_=rows[4 * q : 4 * q + 4, :])
+
+        planes = xT.rearrange("(p j) t -> j p t", j=PACK)
+        for j in range(PACK):
+            cuts = LOAD_CUTS[j]
+            for a, b in zip(cuts, cuts[1:]):
+                nc.sync.dma_start(out=x32[j][:, a:b], in_=planes[j][:, a:b])
+            if j == 0:
+                nc.sync.dma_start(offs_t[:], offs)
+            if j == 1:
+                load_scales(nc.sync, 0)
+        for i in range(3):
+            nc.sync.dma_start(out=w_codes[i][:], in_=words_in[i][0].rearrange("p n t -> p (n t)").bitcast(I32))
+        nc.sync.dma_start(dst_t[:], dst)
+        nc.sync.dma_start(src_t[:], src)
+        load_scales(nc.sync, 1)
+        load_scales(nc.sync, 2)
+
+        for j in range(PACK):
+            cuts = LOAD_CUTS[j]
+            for a, b in zip(cuts, cuts[1:]):
+                nc.vector.tensor_copy(out=x16[j][:, a:b], in_=x32[j][:, a:b])
+            share = VECTOR_SHARE[j]
+            nc.vector.tensor_copy(out=woven[0][:, 0:share, j], in_=x32[j][:].indirect(entries(offs_t, 0, share)))
+            if share < HALF:
+                nc.scalar.activation(woven[0][:, share:HALF, j], x16[j][:].indirect(entries(offs_t, share, HALF)), COPY)
+            nc.scalar.activation(woven[1][:, :, j], x16[j][:].indirect(entries(offs_t, HALF, S)), COPY)
+
+        tables = [[keep.tile([P, S], F32, name="table_%d_%d" % (i, m)) for m in range(N // P)] for i in range(3)]
+
+        def product(i, m, a, b, which):
+            bank = psum.tile([P, BANK], F32, name="bank_%d" % which)
+            nc.tensor.matmul_mx(
+                out=bank[:, 0 : b - a],
+                lhsT=w_codes[i][:, m * P : (m + 1) * P].bitcast(FP8X4),
+                lhsT_scale=w_scales[i][:, m * P : (m + 1) * P],
+                rhs=x_codes[:, a:b].bitcast(FP8X4),
+                rhs_scale=x_scales[:, a:b],
+                start=True,
+                stop=True,
+            )
+            nc.scalar.copy(out=tables[i][m][:, a:b], in_=bank[:, 0 : b - a])
+
+        for a in range(0, S, QUANT):
+            h, c = divmod(a, HALF)
+            nc.vector.quantize_mx(
+                out=x_codes[:, a : a + QUANT].bitcast(FP8X4),
+                scales=x_scales[:, a : a + QUANT],
+                in_=woven[h][:, c : c + QUANT, :].rearrange("p n j -> p (n j)"),
+            )
+            product(0, 0, a, a + QUANT, a // QUANT)
+
+        for m in range(N // P):
+            for i in range(3):
+                if (i, m) != (0, 0):
+                    for a in range(0, S, BANK):
+                        product(i, m, a, a + BANK, 2 + a // BANK)
+            y, e, hh = tables[0][m], tables[1][m], tables[2][m]
+            picked = [keep.tile([P, HALF], F32, name="picked_%d_%d" % (m, u)) for u in range(2)]
+            logits = [keep.tile([P, HALF], F32, name="logits_%d_%d" % (m, u)) for u in range(2)]
+            gates = [keep.tile([P, HALF], F32, name="gates_%d_%d" % (m, u)) for u in range(2)]
+            for u in range(2):
+                nc.vector.tensor_copy(out=picked[u][:], in_=y[:].indirect(entries(dst_t, u * HALF, (u + 1) * HALF)))
+            for u in range(2):
+                nc.vector.tensor_tensor(logits[u][:], e[:].indirect(entries(src_t, u * HALF, (u + 1) * HALF)), picked[u][:], ADD)
+                nc.scalar.activation(gates[u][:], logits[u][:], SIGMOID)
+            cuts = (0, 512, 1024) if m == 0 else (0, 512, 768, 1024)
+            for a, b in zip(cuts, cuts[1:]):
+                u, c = divmod(a, HALF)
+                result = keep.tile([P, b - a], F32, name="result_%d_%d" % (m, a))
+                nc.vector.tensor_tensor(result[:], hh[:].indirect(entries(src_t, a, b)), gates[u][:, c : c + b - a], MULT)
+                nc.sync.dma_start(out=out[m * P : (m + 1) * P, a:b], in_=result[:])

@@ -22,8 +22,9 @@ PACK = 4
 HALF = S // 2
 QUANT = 256
 BANK = 512
-LOAD_CUTS = ((0, 1024, 1536, 2048), (0, 1024, 2048), (0, 1024, 2048), (0, 1024, 1792, 2048))
-VECTOR_SHARE = (256, 256, 512, 512)
+LOAD_CUTS = ((0, 1024, 1536, 2048), (0, 1280, 2048), (0, 1280, 2048), (0, 1024, 1792, 2048))
+VECTOR_SHARE = (320, 320, 384, 384)
+LAST = (384, 640)
 
 
 def entries(lst, a, b):
@@ -36,14 +37,14 @@ def tile_picked_edgeatt_sigmoid_e_kernel(
     nc = tc.nc
     with ExitStack() as ctx:
         keep = ctx.enter_context(tc.tile_pool(name="keep", bufs=1))
-        psum = ctx.enter_context(tc.psum_pool(name="psum", bufs=1))
+        psum = ctx.enter_context(tc.psum_pool(name="psum", bufs=8))
 
         offs_t = keep.tile([P, S // 16], U16, name="offs_t")
         src_t = keep.tile([P, U // 16], U16, name="src_t")
         dst_t = keep.tile([P, U // 16], U16, name="dst_t")
         x32 = [keep.tile([P, T], F32, name="x32_%d" % j) for j in range(PACK)]
         x16 = [keep.tile([P, T], BF16, name="x16_%d" % j) for j in range(PACK)]
-        woven = [keep.tile([P, HALF, PACK], BF16, name="woven_%d" % h, align_bytes=64) for h in range(2)]
+        woven = keep.tile([P, S, PACK], BF16, name="woven", align_bytes=64)
         x_codes = keep.tile([P, S], U32, name="x_codes", align_bytes=64)
         x_scales = keep.tile([P, S], U8, name="x_scales", align_bytes=64)
         w_codes = [keep.tile([P, N], I32, name="w_codes_%d" % i, align_bytes=64) for i in range(3)]
@@ -83,40 +84,41 @@ def tile_picked_edgeatt_sigmoid_e_kernel(
             for a, b in zip(cuts, cuts[1:]):
                 nc.vector.tensor_copy(out=x16[j][:, a:b], in_=x32[j][:, a:b])
             share = VECTOR_SHARE[j]
-            nc.vector.tensor_copy(out=woven[0][:, 0:share, j], in_=x32[j][:].indirect(entries(offs_t, 0, share)))
-            if share < HALF:
-                nc.scalar.activation(woven[0][:, share:HALF, j], x16[j][:].indirect(entries(offs_t, share, HALF)), COPY)
-            nc.scalar.activation(woven[1][:, :, j], x16[j][:].indirect(entries(offs_t, HALF, S)), COPY)
+            nc.vector.tensor_copy(out=woven[:, 0:share, j], in_=x32[j][:].indirect(entries(offs_t, 0, share)))
+            runs = [(share, S)] if j < PACK - 1 else [(LAST[1], S), LAST]
+            for a, b in runs:
+                nc.scalar.activation(woven[:, a:b, j], x16[j][:].indirect(entries(offs_t, a, b)), COPY)
 
         tables = [[keep.tile([P, S], F32, name="table_%d_%d" % (i, m)) for m in range(N // P)] for i in range(3)]
 
-        def product(i, m, a, b, which):
-            bank = psum.tile([P, BANK], F32, name="bank_%d" % which)
-            nc.tensor.matmul_mx(
-                out=bank[:, 0 : b - a],
-                lhsT=w_codes[i][:, m * P : (m + 1) * P].bitcast(FP8X4),
-                lhsT_scale=w_scales[i][:, m * P : (m + 1) * P],
-                rhs=x_codes[:, a:b].bitcast(FP8X4),
-                rhs_scale=x_scales[:, a:b],
-                start=True,
-                stop=True,
-            )
-            nc.scalar.copy(out=tables[i][m][:, a:b], in_=bank[:, 0 : b - a])
+        def product(i, m, cuts, empty):
+            bank = psum.tile([P, BANK], F32, name="bank")
+            for a, b in zip(cuts, cuts[1:]):
+                nc.tensor.matmul_mx(
+                    out=bank[:, a - cuts[0] : b - cuts[0]],
+                    lhsT=w_codes[i][:, m * P : (m + 1) * P].bitcast(FP8X4),
+                    lhsT_scale=w_scales[i][:, m * P : (m + 1) * P],
+                    rhs=x_codes[:, a:b].bitcast(FP8X4),
+                    rhs_scale=x_scales[:, a:b],
+                    start=True,
+                    stop=True,
+                )
+            empty(out=tables[i][m][:, cuts[0] : cuts[-1]], in_=bank[:, 0 : cuts[-1] - cuts[0]])
 
-        for a in range(0, S, QUANT):
-            h, c = divmod(a, HALF)
-            nc.vector.quantize_mx(
-                out=x_codes[:, a : a + QUANT].bitcast(FP8X4),
-                scales=x_scales[:, a : a + QUANT],
-                in_=woven[h][:, c : c + QUANT, :].rearrange("p n j -> p (n j)"),
-            )
-            product(0, 0, a, a + QUANT, a // QUANT)
+        for cuts in ((0, 256, LAST[0]), (LAST[1], LAST[1] + 256, S), LAST):
+            for a, b in zip(cuts, cuts[1:]):
+                nc.vector.quantize_mx(
+                    out=x_codes[:, a:b].bitcast(FP8X4),
+                    scales=x_scales[:, a:b],
+                    in_=woven[:, a:b, :].rearrange("p n j -> p (n j)"),
+                )
+            product(0, 0, cuts, nc.vector.tensor_copy if cuts == LAST else nc.scalar.copy)
+
+        for i, m in ((1, 0), (0, 1), (2, 0), (1, 1), (2, 1)):
+            for a in range(0, S, BANK):
+                product(i, m, (a, a + BANK), nc.scalar.copy)
 
         for m in range(N // P):
-            for i in range(3):
-                if (i, m) != (0, 0):
-                    for a in range(0, S, BANK):
-                        product(i, m, a, a + BANK, 2 + a // BANK)
             y, e, hh = tables[0][m], tables[1][m], tables[2][m]
             picked = [keep.tile([P, HALF], F32, name="picked_%d_%d" % (m, u)) for u in range(2)]
             logits = [keep.tile([P, HALF], F32, name="logits_%d_%d" % (m, u)) for u in range(2)]

@@ -22,7 +22,8 @@ PACK = 4
 HALF = S // 2
 QUANT = 256
 BANK = 512
-LOAD_CUTS = ((0, 1024, 1536, 2048), (0, 1280, 2048), (0, 1280, 2048), (0, 1024, 1792, 2048))
+LOAD_CUTS = ((0, 1280, 2048), (0, 1280, 2048), (0, 1280, 2048), (0, 1024, 1792, 2048))
+ORDER = (2, 0, 1, 3)
 VECTOR_SHARE = (320, 320, 384, 384)
 LAST = (384, 640)
 
@@ -64,13 +65,13 @@ def tile_picked_edgeatt_sigmoid_e_kernel(
                 queue.dma_start(out=w_scales[i][32 * q : 32 * q + 4, :].bitcast(I32), in_=rows[4 * q : 4 * q + 4, :])
 
         planes = xT.rearrange("(p j) t -> j p t", j=PACK)
-        for j in range(PACK):
+        for j in ORDER:
             cuts = LOAD_CUTS[j]
             for a, b in zip(cuts, cuts[1:]):
                 nc.sync.dma_start(out=x32[j][:, a:b], in_=planes[j][:, a:b])
-            if j == 0:
+            if j == ORDER[0]:
                 nc.sync.dma_start(offs_t[:], offs)
-            if j == 1:
+            if j == ORDER[1]:
                 load_scales(nc.sync, 0)
         for i in range(3):
             nc.sync.dma_start(out=w_codes[i][:], in_=words_in[i][0].rearrange("p n t -> p (n t)").bitcast(I32))
@@ -79,7 +80,7 @@ def tile_picked_edgeatt_sigmoid_e_kernel(
         load_scales(nc.sync, 1)
         load_scales(nc.sync, 2)
 
-        for j in range(PACK):
+        for j in ORDER:
             cuts = LOAD_CUTS[j]
             for a, b in zip(cuts, cuts[1:]):
                 nc.vector.tensor_copy(out=x16[j][:, a:b], in_=x32[j][:, a:b])
@@ -105,14 +106,16 @@ def tile_picked_edgeatt_sigmoid_e_kernel(
                 )
             empty(out=tables[i][m][:, cuts[0] : cuts[-1]], in_=bank[:, 0 : cuts[-1] - cuts[0]])
 
-        for cuts in ((0, 256, LAST[0]), (LAST[1], LAST[1] + 256, S), LAST):
+        pieces = ((0, 256, LAST[0]), (LAST[1], LAST[1] + 256, S), (LAST[0], HALF), (HALF, LAST[1]))
+        for cuts in pieces:
             for a, b in zip(cuts, cuts[1:]):
                 nc.vector.quantize_mx(
                     out=x_codes[:, a:b].bitcast(FP8X4),
                     scales=x_scales[:, a:b],
                     in_=woven[:, a:b, :].rearrange("p n j -> p (n j)"),
                 )
-            product(0, 0, cuts, nc.vector.tensor_copy if cuts == LAST else nc.scalar.copy)
+        for cuts in pieces:
+            product(0, 0, cuts, nc.vector.tensor_copy if cuts[-1] == S else nc.scalar.copy)
 
         for i, m in ((1, 0), (0, 1), (2, 0), (1, 1), (2, 1)):
             for a in range(0, S, BANK):
@@ -128,7 +131,7 @@ def tile_picked_edgeatt_sigmoid_e_kernel(
             for u in range(2):
                 nc.vector.tensor_tensor(logits[u][:], e[:].indirect(entries(src_t, u * HALF, (u + 1) * HALF)), picked[u][:], ADD)
                 nc.scalar.activation(gates[u][:], logits[u][:], SIGMOID)
-            cuts = (0, 512, 1024) if m == 0 else (0, 512, 768, 1024)
+            cuts = (0, 512, 1024) if m == 0 else (0, 512, 832, 1024)
             for a, b in zip(cuts, cuts[1:]):
                 u, c = divmod(a, HALF)
                 result = keep.tile([P, b - a], F32, name="result_%d_%d" % (m, a))

@@ -22,10 +22,11 @@ PACK = 4
 HALF = S // 2
 QUANT = 256
 BANK = 512
-LOAD_CUTS = ((0, 1280, 2048), (0, 1280, 2048), (0, 1280, 2048), (0, 1024, 1792, 2048))
+LOAD_CUTS = ((0, 896, 2048), (0, 896, 2048), (0, 2048), (0, 768, 1664, 2048))
 ORDER = (2, 0, 1, 3)
-VECTOR_SHARE = (320, 320, 384, 384)
+VECTOR_SHARE = (416, 416, 384, 384)
 LAST = (384, 640)
+WINDOW = (1376, 1040, 1024)
 
 
 def entries(lst, a, b):
@@ -71,10 +72,10 @@ def tile_picked_edgeatt_sigmoid_e_kernel(
                 nc.sync.dma_start(out=x32[j][:, a:b], in_=planes[j][:, a:b])
             if j == ORDER[0]:
                 nc.sync.dma_start(offs_t[:], offs)
-            if j == ORDER[1]:
-                load_scales(nc.sync, 0)
         for i in range(3):
             nc.sync.dma_start(out=w_codes[i][:], in_=words_in[i][0].rearrange("p n t -> p (n t)").bitcast(I32))
+            if i == 0:
+                load_scales(nc.sync, 0)
         nc.sync.dma_start(dst_t[:], dst)
         nc.sync.dma_start(src_t[:], src)
         load_scales(nc.sync, 1)
@@ -82,15 +83,19 @@ def tile_picked_edgeatt_sigmoid_e_kernel(
 
         for j in ORDER:
             cuts = LOAD_CUTS[j]
+            if j == ORDER[0]:
+                cuts = (0, 1376)
+                nc.scalar.copy(out=x16[j][:, 1376:T], in_=x32[j][:, 1376:T])
             for a, b in zip(cuts, cuts[1:]):
-                nc.vector.tensor_copy(out=x16[j][:, a:b], in_=x32[j][:, a:b])
+                engine = nc.gpsimd if a == 0 and j != ORDER[0] else nc.vector
+                engine.tensor_copy(out=x16[j][:, a:b], in_=x32[j][:, a:b])
             share = VECTOR_SHARE[j]
             nc.vector.tensor_copy(out=woven[:, 0:share, j], in_=x32[j][:].indirect(entries(offs_t, 0, share)))
             runs = [(share, S)] if j < PACK - 1 else [(LAST[1], S), LAST]
             for a, b in runs:
                 nc.scalar.activation(woven[:, a:b, j], x16[j][:].indirect(entries(offs_t, a, b)), COPY)
 
-        tables = [[keep.tile([P, S], F32, name="table_%d_%d" % (i, m)) for m in range(N // P)] for i in range(3)]
+        tables = [[keep.tile([P, WINDOW[i]], F32, name="table_%d_%d" % (i, m)) for m in range(N // P)] for i in range(3)]
 
         def product(i, m, cuts, empty):
             bank = psum.tile([P, BANK], F32, name="bank")
@@ -117,23 +122,22 @@ def tile_picked_edgeatt_sigmoid_e_kernel(
         for cuts in pieces:
             product(0, 0, cuts, nc.vector.tensor_copy if cuts[-1] == S else nc.scalar.copy)
 
-        for i, m in ((1, 0), (0, 1), (2, 0), (1, 1), (2, 1)):
+        for i, m in ((0, 1), (1, 0), (1, 1), (2, 0), (2, 1)):
             for a in range(0, S, BANK):
                 product(i, m, (a, a + BANK), nc.scalar.copy)
 
-        for m in range(N // P):
-            y, e, hh = tables[0][m], tables[1][m], tables[2][m]
-            picked = [keep.tile([P, HALF], F32, name="picked_%d_%d" % (m, u)) for u in range(2)]
-            logits = [keep.tile([P, HALF], F32, name="logits_%d_%d" % (m, u)) for u in range(2)]
-            gates = [keep.tile([P, HALF], F32, name="gates_%d_%d" % (m, u)) for u in range(2)]
-            for u in range(2):
-                nc.vector.tensor_copy(out=picked[u][:], in_=y[:].indirect(entries(dst_t, u * HALF, (u + 1) * HALF)))
-            for u in range(2):
-                nc.vector.tensor_tensor(logits[u][:], e[:].indirect(entries(src_t, u * HALF, (u + 1) * HALF)), picked[u][:], ADD)
-                nc.scalar.activation(gates[u][:], logits[u][:], SIGMOID)
+        blocks = range(N // P)
+        picked = [keep.tile([P, U], F32, name="picked_%d" % m) for m in blocks]
+        logits = [keep.tile([P, U], F32, name="logits_%d" % m) for m in blocks]
+        gates = [keep.tile([P, U], F32, name="gates_%d" % m) for m in blocks]
+        for m in blocks:
+            nc.vector.tensor_copy(out=picked[m][:], in_=tables[0][m][:].indirect(dst_t[:]))
+        for m in blocks:
+            nc.vector.tensor_tensor(logits[m][:], tables[1][m][:].indirect(src_t[:]), picked[m][:], ADD)
+            nc.scalar.activation(gates[m][:], logits[m][:], SIGMOID)
+        for m in blocks:
             cuts = (0, 512, 1024) if m == 0 else (0, 512, 832, 1024)
             for a, b in zip(cuts, cuts[1:]):
-                u, c = divmod(a, HALF)
                 result = keep.tile([P, b - a], F32, name="result_%d_%d" % (m, a))
-                nc.vector.tensor_tensor(result[:], hh[:].indirect(entries(src_t, a, b)), gates[u][:, c : c + b - a], MULT)
+                nc.vector.tensor_tensor(result[:], tables[2][m][:].indirect(entries(src_t, a, b)), gates[m][:, a:b], MULT)
                 nc.sync.dma_start(out=out[m * P : (m + 1) * P, a:b], in_=result[:])

@@ -22,9 +22,9 @@ PACK = 4
 HALF = S // 2
 QUANT = 256
 BANK = 512
-LOAD_CUTS = ((0, 896, 2048), (0, 896, 2048), (0, 2048), (0, 768, 1664, 2048))
+LOAD_CUTS = ((0, 896, 2048), (0, 640, 1280, 2048), (0, 2048), (0, 768, 1664, 2048))
 ORDER = (2, 0, 1, 3)
-VECTOR_SHARE = (416, 416, 384, 384)
+VECTOR_SHARE = (384, 384, 384, 384)
 LAST = (384, 640)
 WINDOW = (1376, 1040, 1024)
 
@@ -87,7 +87,7 @@ def tile_picked_edgeatt_sigmoid_e_kernel(
                 cuts = (0, 1376)
                 nc.scalar.copy(out=x16[j][:, 1376:T], in_=x32[j][:, 1376:T])
             for a, b in zip(cuts, cuts[1:]):
-                engine = nc.gpsimd if a == 0 and j != ORDER[0] else nc.vector
+                engine = nc.gpsimd if b <= 1280 else nc.vector
                 engine.tensor_copy(out=x16[j][:, a:b], in_=x32[j][:, a:b])
             share = VECTOR_SHARE[j]
             nc.vector.tensor_copy(out=woven[:, 0:share, j], in_=x32[j][:].indirect(entries(offs_t, 0, share)))

@@ -19,18 +19,24 @@ SIGMOID = mybir.ActivationFunctionType.Sigmoid
 
 P = 128
 PACK = 4
-HALF = S // 2
-QUANT = 256
 BANK = 512
-LOAD_CUTS = ((0, 896, 2048), (0, 640, 1280, 2048), (0, 2048), (0, 768, 1664, 2048))
-ORDER = (2, 0, 1, 3)
-VECTOR_SHARE = (384, 384, 384, 384)
-LAST = (384, 640)
-WINDOW = (1376, 1040, 1024)
+Y, E, H = 0, 1, 2
+
+LOAD_CUTS = ((0, T), (0, 896, T), (0, 640, 1280, T), (0, 768, 1664, T))
+GPSIMD_END = 1280
+FIRST_SPLIT = 1376
+VECTOR_SHARE = 384
+LAST = (VECTOR_SHARE, VECTOR_SHARE + 256)
+WINDOW = (1376, 1040, S)
+STORE_CUTS = ((0, 512, U), (0, 512, 832, U))
 
 
 def entries(lst, a, b):
     return lst[:, a // 16 : b // 16]
+
+
+def spans(cuts):
+    return zip(cuts, cuts[1:])
 
 
 def tile_picked_edgeatt_sigmoid_e_kernel(
@@ -49,57 +55,59 @@ def tile_picked_edgeatt_sigmoid_e_kernel(
         woven = keep.tile([P, S, PACK], BF16, name="woven", align_bytes=64)
         x_codes = keep.tile([P, S], U32, name="x_codes", align_bytes=64)
         x_scales = keep.tile([P, S], U8, name="x_scales", align_bytes=64)
-        w_codes = [keep.tile([P, N], I32, name="w_codes_%d" % i, align_bytes=64) for i in range(3)]
-        w_scales = [keep.tile([P, N], U8, name="w_scales_%d" % i, align_bytes=64) for i in range(3)]
+        w_codes = [keep.tile([P, N], I32, name="w_codes_%d" % i, align_bytes=64) for i in (Y, E, H)]
+        w_scales = [keep.tile([P, N], U8, name="w_scales_%d" % i, align_bytes=64) for i in (Y, E, H)]
         words_in = (w1_words, w2_words, w3_words)
         scales_in = (w1_scales, w2_scales, w3_scales)
 
-        for i in range(3):
+        for i in (Y, E, H):
             nc.vector.memset(w_scales[i][:].bitcast(I32), 0)
+
         warm = keep.tile([P, 2], F32, name="warm")
         nc.vector.memset(warm[:, 0:1], 0.0)
         nc.scalar.activation(warm[:, 1:2], warm[:, 0:1], SIGMOID)
 
-        def load_scales(queue, i):
+        def load_scales(i):
             rows = scales_in[i][0].bitcast(I32)
             for q in range(4):
-                queue.dma_start(out=w_scales[i][32 * q : 32 * q + 4, :].bitcast(I32), in_=rows[4 * q : 4 * q + 4, :])
+                nc.sync.dma_start(out=w_scales[i][32 * q : 32 * q + 4, :].bitcast(I32), in_=rows[4 * q : 4 * q + 4, :])
 
         planes = xT.rearrange("(p j) t -> j p t", j=PACK)
-        for j in ORDER:
-            cuts = LOAD_CUTS[j]
-            for a, b in zip(cuts, cuts[1:]):
+        for j in range(PACK):
+            for a, b in spans(LOAD_CUTS[j]):
                 nc.sync.dma_start(out=x32[j][:, a:b], in_=planes[j][:, a:b])
-            if j == ORDER[0]:
+            if j == 0:
                 nc.sync.dma_start(offs_t[:], offs)
-        for i in range(3):
+        for i in (Y, E, H):
             nc.sync.dma_start(out=w_codes[i][:], in_=words_in[i][0].rearrange("p n t -> p (n t)").bitcast(I32))
-            if i == 0:
-                load_scales(nc.sync, 0)
+            if i == Y:
+                load_scales(Y)
         nc.sync.dma_start(dst_t[:], dst)
         nc.sync.dma_start(src_t[:], src)
-        load_scales(nc.sync, 1)
-        load_scales(nc.sync, 2)
+        load_scales(E)
+        load_scales(H)
 
-        for j in ORDER:
-            cuts = LOAD_CUTS[j]
-            if j == ORDER[0]:
-                cuts = (0, 1376)
-                nc.scalar.copy(out=x16[j][:, 1376:T], in_=x32[j][:, 1376:T])
-            for a, b in zip(cuts, cuts[1:]):
-                engine = nc.gpsimd if b <= 1280 else nc.vector
-                engine.tensor_copy(out=x16[j][:, a:b], in_=x32[j][:, a:b])
-            share = VECTOR_SHARE[j]
-            nc.vector.tensor_copy(out=woven[:, 0:share, j], in_=x32[j][:].indirect(entries(offs_t, 0, share)))
-            runs = [(share, S)] if j < PACK - 1 else [(LAST[1], S), LAST]
+        for j in range(PACK):
+            if j == 0:
+                nc.scalar.copy(out=x16[j][:, FIRST_SPLIT:T], in_=x32[j][:, FIRST_SPLIT:T])
+                nc.vector.tensor_copy(out=x16[j][:, 0:FIRST_SPLIT], in_=x32[j][:, 0:FIRST_SPLIT])
+            else:
+                for a, b in spans(LOAD_CUTS[j]):
+                    engine = nc.gpsimd if b <= GPSIMD_END else nc.vector
+                    engine.tensor_copy(out=x16[j][:, a:b], in_=x32[j][:, a:b])
+            nc.vector.tensor_copy(
+                out=woven[:, 0:VECTOR_SHARE, j], in_=x32[j][:].indirect(entries(offs_t, 0, VECTOR_SHARE))
+            )
+            runs = [(VECTOR_SHARE, S)] if j < PACK - 1 else [(LAST[1], S), LAST]
             for a, b in runs:
                 nc.scalar.activation(woven[:, a:b, j], x16[j][:].indirect(entries(offs_t, a, b)), COPY)
 
-        tables = [[keep.tile([P, WINDOW[i]], F32, name="table_%d_%d" % (i, m)) for m in range(N // P)] for i in range(3)]
+        blocks = range(N // P)
+        tables = [[keep.tile([P, WINDOW[i]], F32, name="table_%d_%d" % (i, m)) for m in blocks] for i in (Y, E, H)]
 
         def product(i, m, cuts, empty):
             bank = psum.tile([P, BANK], F32, name="bank")
-            for a, b in zip(cuts, cuts[1:]):
+            for a, b in spans(cuts):
                 nc.tensor.matmul_mx(
                     out=bank[:, a - cuts[0] : b - cuts[0]],
                     lhsT=w_codes[i][:, m * P : (m + 1) * P].bitcast(FP8X4),
@@ -111,33 +119,31 @@ def tile_picked_edgeatt_sigmoid_e_kernel(
                 )
             empty(out=tables[i][m][:, cuts[0] : cuts[-1]], in_=bank[:, 0 : cuts[-1] - cuts[0]])
 
-        pieces = ((0, 256, LAST[0]), (LAST[1], LAST[1] + 256, S), (LAST[0], HALF), (HALF, LAST[1]))
+        pieces = ((0, 256, LAST[0]), (LAST[1], LAST[1] + 256, S), (LAST[0], BANK), (BANK, LAST[1]))
         for cuts in pieces:
-            for a, b in zip(cuts, cuts[1:]):
+            for a, b in spans(cuts):
                 nc.vector.quantize_mx(
                     out=x_codes[:, a:b].bitcast(FP8X4),
                     scales=x_scales[:, a:b],
                     in_=woven[:, a:b, :].rearrange("p n j -> p (n j)"),
                 )
         for cuts in pieces:
-            product(0, 0, cuts, nc.vector.tensor_copy if cuts[-1] == S else nc.scalar.copy)
+            product(Y, 0, cuts, nc.vector.tensor_copy if cuts[-1] == S else nc.scalar.copy)
 
-        for i, m in ((0, 1), (1, 0), (1, 1), (2, 0), (2, 1)):
+        for i, m in ((Y, 1), (E, 0), (E, 1), (H, 0), (H, 1)):
             for a in range(0, S, BANK):
                 product(i, m, (a, a + BANK), nc.scalar.copy)
 
-        blocks = range(N // P)
         picked = [keep.tile([P, U], F32, name="picked_%d" % m) for m in blocks]
         logits = [keep.tile([P, U], F32, name="logits_%d" % m) for m in blocks]
         gates = [keep.tile([P, U], F32, name="gates_%d" % m) for m in blocks]
         for m in blocks:
-            nc.vector.tensor_copy(out=picked[m][:], in_=tables[0][m][:].indirect(dst_t[:]))
+            nc.vector.tensor_copy(out=picked[m][:], in_=tables[Y][m][:].indirect(dst_t[:]))
         for m in blocks:
-            nc.vector.tensor_tensor(logits[m][:], tables[1][m][:].indirect(src_t[:]), picked[m][:], ADD)
+            nc.vector.tensor_tensor(logits[m][:], tables[E][m][:].indirect(src_t[:]), picked[m][:], ADD)
             nc.scalar.activation(gates[m][:], logits[m][:], SIGMOID)
         for m in blocks:
-            cuts = (0, 512, 1024) if m == 0 else (0, 512, 832, 1024)
-            for a, b in zip(cuts, cuts[1:]):
+            for a, b in spans(STORE_CUTS[m]):
                 result = keep.tile([P, b - a], F32, name="result_%d_%d" % (m, a))
-                nc.vector.tensor_tensor(result[:], tables[2][m][:].indirect(entries(src_t, a, b)), gates[m][:, a:b], MULT)
+                nc.vector.tensor_tensor(result[:], tables[H][m][:].indirect(entries(src_t, a, b)), gates[m][:, a:b], MULT)
                 nc.sync.dma_start(out=out[m * P : (m + 1) * P, a:b], in_=result[:])

@@ -25,7 +25,9 @@ Y, E, H = 0, 1, 2
 LOAD_CUTS = ((0, T), (0, 896, T), (0, 640, 1280, T), (0, 768, 1664, T))
 GPSIMD_END = 1280
 FIRST_SPLIT = 1376
-VECTOR_SHARE = 384
+VECTOR_SHARE = 448
+MIDDLE_SHARE = 384
+ORDER = (2, 0, 1, 3)
 LAST = (VECTOR_SHARE, VECTOR_SHARE + 256)
 WINDOW = (1376, 1040, S)
 STORE_CUTS = ((0, 512, U), (0, 512, 832, U))
@@ -73,10 +75,10 @@ def tile_picked_edgeatt_sigmoid_e_kernel(
                 nc.sync.dma_start(out=w_scales[i][32 * q : 32 * q + 4, :].bitcast(I32), in_=rows[4 * q : 4 * q + 4, :])
 
         planes = xT.rearrange("(p j) t -> j p t", j=PACK)
-        for j in range(PACK):
-            for a, b in spans(LOAD_CUTS[j]):
+        for turn, j in enumerate(ORDER):
+            for a, b in spans(LOAD_CUTS[turn]):
                 nc.sync.dma_start(out=x32[j][:, a:b], in_=planes[j][:, a:b])
-            if j == 0:
+            if turn == 0:
                 nc.sync.dma_start(offs_t[:], offs)
         for i in (Y, E, H):
             nc.sync.dma_start(out=w_codes[i][:], in_=words_in[i][0].rearrange("p n t -> p (n t)").bitcast(I32))
@@ -87,18 +89,17 @@ def tile_picked_edgeatt_sigmoid_e_kernel(
         load_scales(E)
         load_scales(H)
 
-        for j in range(PACK):
-            if j == 0:
+        for turn, j in enumerate(ORDER):
+            if turn == 0:
                 nc.scalar.copy(out=x16[j][:, FIRST_SPLIT:T], in_=x32[j][:, FIRST_SPLIT:T])
                 nc.vector.tensor_copy(out=x16[j][:, 0:FIRST_SPLIT], in_=x32[j][:, 0:FIRST_SPLIT])
             else:
-                for a, b in spans(LOAD_CUTS[j]):
+                for a, b in spans(LOAD_CUTS[turn]):
                     engine = nc.gpsimd if b <= GPSIMD_END else nc.vector
                     engine.tensor_copy(out=x16[j][:, a:b], in_=x32[j][:, a:b])
-            nc.vector.tensor_copy(
-                out=woven[:, 0:VECTOR_SHARE, j], in_=x32[j][:].indirect(entries(offs_t, 0, VECTOR_SHARE))
-            )
-            runs = [(VECTOR_SHARE, S)] if j < PACK - 1 else [(LAST[1], S), LAST]
+            share = MIDDLE_SHARE if j < 2 else VECTOR_SHARE
+            nc.vector.tensor_copy(out=woven[:, 0:share, j], in_=x32[j][:].indirect(entries(offs_t, 0, share)))
+            runs = [(share, S)] if j < PACK - 1 else [(LAST[1], S), LAST]
             for a, b in runs:
                 nc.scalar.activation(woven[:, a:b, j], x16[j][:].indirect(entries(offs_t, a, b)), COPY)
 
@@ -119,7 +120,7 @@ def tile_picked_edgeatt_sigmoid_e_kernel(
                 )
             empty(out=tables[i][m][:, cuts[0] : cuts[-1]], in_=bank[:, 0 : cuts[-1] - cuts[0]])
 
-        pieces = ((0, 256, LAST[0]), (LAST[1], LAST[1] + 256, S), (LAST[0], BANK), (BANK, LAST[1]))
+        pieces = ((0, 256, 384, LAST[0]), (LAST[1], LAST[1] + 256, S), (LAST[0], LAST[0] + 128), (LAST[0] + 128, LAST[1]))
         for cuts in pieces:
             for a, b in spans(cuts):
                 nc.vector.quantize_mx(

@@ -47,7 +47,7 @@ def tile_picked_edgeatt_sigmoid_e_kernel(
     nc = tc.nc
     with ExitStack() as ctx:
         keep = ctx.enter_context(tc.tile_pool(name="keep", bufs=1))
-        psum = ctx.enter_context(tc.psum_pool(name="psum", bufs=8))
+        psum = ctx.enter_context(tc.psum_pool(name="psum", bufs=1))
 
         offs_t = keep.tile([P, S // 16], U16, name="offs_t")
         src_t = keep.tile([P, U // 16], U16, name="src_t")
@@ -95,19 +95,18 @@ def tile_picked_edgeatt_sigmoid_e_kernel(
                 nc.vector.tensor_copy(out=x16[j][:, 0:FIRST_SPLIT], in_=x32[j][:, 0:FIRST_SPLIT])
             else:
                 for a, b in spans(LOAD_CUTS[turn]):
-                    engine = nc.gpsimd if b <= GPSIMD_END else nc.vector
+                    engine = nc.gpsimd if b <= GPSIMD_END or (j, b) == (PACK - 1, T) else nc.vector
                     engine.tensor_copy(out=x16[j][:, a:b], in_=x32[j][:, a:b])
-            share = MIDDLE_SHARE if j < 2 else VECTOR_SHARE
-            nc.vector.tensor_copy(out=woven[:, 0:share, j], in_=x32[j][:].indirect(entries(offs_t, 0, share)))
-            runs = [(share, S)] if j < PACK - 1 else [(LAST[1], S), LAST]
-            for a, b in runs:
+            for a, b in [(0, MIDDLE_SHARE)] if j < 2 else [(0, 256), (256, 512)]:
+                nc.vector.tensor_copy(out=woven[:, a:b, j], in_=x32[j][:].indirect(entries(offs_t, a, b)))
+            for a, b in [(MIDDLE_SHARE, S)] if j < 2 else [(512, 768), (768, S)]:
                 nc.scalar.activation(woven[:, a:b, j], x16[j][:].indirect(entries(offs_t, a, b)), COPY)
 
         blocks = range(N // P)
         tables = [[keep.tile([P, WINDOW[i]], F32, name="table_%d_%d" % (i, m)) for m in blocks] for i in (Y, E, H)]
 
-        def product(i, m, cuts, empty):
-            bank = psum.tile([P, BANK], F32, name="bank")
+        def product(i, m, cuts, number, empty=nc.scalar.copy):
+            bank = psum.tile([P, BANK], F32, name="bank_%d" % number)
             for a, b in spans(cuts):
                 nc.tensor.matmul_mx(
                     out=bank[:, a - cuts[0] : b - cuts[0]],
@@ -120,7 +119,7 @@ def tile_picked_edgeatt_sigmoid_e_kernel(
                 )
             empty(out=tables[i][m][:, cuts[0] : cuts[-1]], in_=bank[:, 0 : cuts[-1] - cuts[0]])
 
-        pieces = ((0, 256, 384, LAST[0]), (LAST[1], LAST[1] + 256, S), (LAST[0], LAST[0] + 128), (LAST[0] + 128, LAST[1]))
+        pieces = ((0, 256), (512, 768), (256, 512), (768, 896), (896, S))
         for cuts in pieces:
             for a, b in spans(cuts):
                 nc.vector.quantize_mx(
@@ -128,12 +127,13 @@ def tile_picked_edgeatt_sigmoid_e_kernel(
                     scales=x_scales[:, a:b],
                     in_=woven[:, a:b, :].rearrange("p n j -> p (n j)"),
                 )
-        for cuts in pieces:
-            product(Y, 0, cuts, nc.vector.tensor_copy if cuts[-1] == S else nc.scalar.copy)
+        for number, cuts in enumerate(pieces):
+            product(Y, 0, cuts, number, nc.vector.tensor_copy if number == 2 else nc.scalar.copy)
 
-        for i, m in ((Y, 1), (E, 0), (E, 1), (H, 0), (H, 1)):
-            for a in range(0, S, BANK):
-                product(i, m, (a, a + BANK), nc.scalar.copy)
+        numbers = ((5, 3), (6, 4), (7, 5), (3, 6), (4, 7))
+        for (i, m), (late, early) in zip(((Y, 1), (E, 0), (E, 1), (H, 0), (H, 1)), numbers):
+            product(i, m, (BANK, S), late)
+            product(i, m, (0, BANK), early)
 
         picked = [keep.tile([P, U], F32, name="picked_%d" % m) for m in blocks]
         logits = [keep.tile([P, U], F32, name="logits_%d" % m) for m in blocks]

@@ -25,7 +25,7 @@ Y, E, H = 0, 1, 2
 LOAD_CUTS = ((0, T), (0, 896, T), (0, 640, 1280, T), (0, 768, 1664, T))
 GPSIMD_END = 1280
 FIRST_SPLIT = 1376
-VECTOR_SHARE = 448
+VECTOR_SHARE = 480
 MIDDLE_SHARE = 384
 ORDER = (2, 0, 1, 3)
 LAST = (VECTOR_SHARE, VECTOR_SHARE + 256)
@@ -97,9 +97,9 @@ def tile_picked_edgeatt_sigmoid_e_kernel(
                 for a, b in spans(LOAD_CUTS[turn]):
                     engine = nc.gpsimd if b <= GPSIMD_END or (j, b) == (PACK - 1, T) else nc.vector
                     engine.tensor_copy(out=x16[j][:, a:b], in_=x32[j][:, a:b])
-            for a, b in [(0, MIDDLE_SHARE)] if j < 2 else [(0, 256), (256, 512)]:
+            for a, b in [(0, MIDDLE_SHARE)] if j < 2 else [(0, VECTOR_SHARE)]:
                 nc.vector.tensor_copy(out=woven[:, a:b, j], in_=x32[j][:].indirect(entries(offs_t, a, b)))
-            for a, b in [(MIDDLE_SHARE, S)] if j < 2 else [(512, 768), (768, S)]:
+            for a, b in [(MIDDLE_SHARE, S)] if j < 2 else [(VECTOR_SHARE, 768), (768, S)]:
                 nc.scalar.activation(woven[:, a:b, j], x16[j][:].indirect(entries(offs_t, a, b)), COPY)
 
         blocks = range(N // P)
@@ -119,7 +119,7 @@ def tile_picked_edgeatt_sigmoid_e_kernel(
                 )
             empty(out=tables[i][m][:, cuts[0] : cuts[-1]], in_=bank[:, 0 : cuts[-1] - cuts[0]])
 
-        pieces = ((0, 256), (512, 768), (256, 512), (768, 896), (896, S))
+        pieces = ((0, 256), (256, 512), (512, 768), (768, 896), (896, S))
         for cuts in pieces:
             for a, b in spans(cuts):
                 nc.vector.quantize_mx(

@@ -22,7 +22,7 @@ PACK = 4
 BANK = 512
 Y, E, H = 0, 1, 2
 
-LOAD_CUTS = ((0, T), (0, 896, T), (0, 640, 1280, T), (0, 768, 1664, T))
+LOAD_CUTS = ((0, T), (0, 896, T), (0, 896, T), (0, 768, 1664, T))
 GPSIMD_END = 1280
 FIRST_SPLIT = 1376
 VECTOR_SHARE = 480
@@ -30,7 +30,7 @@ MIDDLE_SHARE = 384
 ORDER = (2, 0, 1, 3)
 LAST = (VECTOR_SHARE, VECTOR_SHARE + 256)
 WINDOW = (1376, 1040, S)
-STORE_CUTS = ((0, 512, U), (0, 512, 832, U))
+STORE_CUTS = ((0, 512, U), (0, 384, 704, 896, U))
 
 
 def entries(lst, a, b):

@@ -80,10 +80,9 @@ def tile_picked_edgeatt_sigmoid_e_kernel(
                 nc.sync.dma_start(out=x32[j][:, a:b], in_=planes[j][:, a:b])
             if turn == 0:
                 nc.sync.dma_start(offs_t[:], offs)
+                load_scales(Y)
         for i in (Y, E, H):
             nc.sync.dma_start(out=w_codes[i][:], in_=words_in[i][0].rearrange("p n t -> p (n t)").bitcast(I32))
-            if i == Y:
-                load_scales(Y)
         nc.sync.dma_start(dst_t[:], dst)
         nc.sync.dma_start(src_t[:], src)
         load_scales(E)

@@ -29,7 +29,7 @@ VECTOR_SHARE = 480
 MIDDLE_SHARE = 384
 ORDER = (2, 0, 1, 3)
 LAST = (VECTOR_SHARE, VECTOR_SHARE + 256)
-WINDOW = (1376, 1040, S)
+WINDOW = ((1376, S), (1040, S), (S, S))
 STORE_CUTS = ((0, 512, U), (0, 384, 704, 896, U))
 
 
@@ -54,7 +54,7 @@ def tile_picked_edgeatt_sigmoid_e_kernel(
         dst_t = keep.tile([P, U // 16], U16, name="dst_t")
         x32 = [keep.tile([P, T], F32, name="x32_%d" % j) for j in range(PACK)]
         x16 = [keep.tile([P, T], BF16, name="x16_%d" % j) for j in range(PACK)]
-        woven = keep.tile([P, S, PACK], BF16, name="woven", align_bytes=64)
+        woven = keep.tile([P, S, PACK], BF16, name="woven", tag="woven", align_bytes=64)
         x_codes = keep.tile([P, S], U32, name="x_codes", align_bytes=64)
         x_scales = keep.tile([P, S], U8, name="x_scales", align_bytes=64)
         w_codes = [keep.tile([P, N], I32, name="w_codes_%d" % i, align_bytes=64) for i in (Y, E, H)]
@@ -102,48 +102,85 @@ def tile_picked_edgeatt_sigmoid_e_kernel(
                 nc.scalar.activation(woven[:, a:b, j], x16[j][:].indirect(entries(offs_t, a, b)), COPY)
 
         blocks = range(N // P)
-        tables = [[keep.tile([P, WINDOW[i]], F32, name="table_%d_%d" % (i, m)) for m in blocks] for i in (Y, E, H)]
+        tables = [[keep.tile([P, WINDOW[i][m]], F32, name="table_%d_%d" % (i, m)) if (i, m) != (Y, 1) else None for m in blocks] for i in (Y, E, H)]
 
-        def product(i, m, cuts, number, empty=nc.scalar.copy):
+        def one_pass(target, i, m, a, b):
+            nc.tensor.matmul_mx(
+                out=target,
+                lhsT=w_codes[i][:, m * P : (m + 1) * P].bitcast(FP8X4),
+                lhsT_scale=w_scales[i][:, m * P : (m + 1) * P],
+                rhs=x_codes[:, a:b].bitcast(FP8X4),
+                rhs_scale=x_scales[:, a:b],
+                start=True,
+                stop=True,
+            )
+
+        def product(i, m, cuts, number):
+            a, b = cuts
             bank = psum.tile([P, BANK], F32, name="bank_%d" % number)
-            for a, b in spans(cuts):
-                nc.tensor.matmul_mx(
-                    out=bank[:, a - cuts[0] : b - cuts[0]],
-                    lhsT=w_codes[i][:, m * P : (m + 1) * P].bitcast(FP8X4),
-                    lhsT_scale=w_scales[i][:, m * P : (m + 1) * P],
-                    rhs=x_codes[:, a:b].bitcast(FP8X4),
-                    rhs_scale=x_scales[:, a:b],
-                    start=True,
-                    stop=True,
-                )
-            empty(out=tables[i][m][:, cuts[0] : cuts[-1]], in_=bank[:, 0 : cuts[-1] - cuts[0]])
+            one_pass(bank[:, 0 : b - a], i, m, a, b)
+            return lambda copy: copy(out=tables[i][m][:, a:b], in_=bank[:, 0 : b - a])
 
         pieces = ((0, 256), (256, 512), (512, 768), (768, 896), (896, S))
-        for cuts in pieces:
-            for a, b in spans(cuts):
-                nc.vector.quantize_mx(
-                    out=x_codes[:, a:b].bitcast(FP8X4),
-                    scales=x_scales[:, a:b],
-                    in_=woven[:, a:b, :].rearrange("p n j -> p (n j)"),
-                )
-        for number, cuts in enumerate(pieces):
-            product(Y, 0, cuts, number, nc.vector.tensor_copy if number == 2 else nc.scalar.copy)
+        for a, b in pieces:
+            nc.vector.quantize_mx(
+                out=x_codes[:, a:b].bitcast(FP8X4),
+                scales=x_scales[:, a:b],
+                in_=woven[:, a:b, :].rearrange("p n j -> p (n j)"),
+            )
+        tables[Y][1] = keep.tile([P, S], F32, name="table_y1", tag="woven", align_bytes=64)
+        quarters = tables[Y][1][:].rearrange("p (h q n) -> p q h n", h=2, q=2)
 
-        numbers = ((5, 3), (6, 4), (7, 5), (3, 6), (4, 7))
-        for (i, m), (late, early) in zip(((Y, 1), (E, 0), (E, 1), (H, 0), (H, 1)), numbers):
-            product(i, m, (BANK, S), late)
-            product(i, m, (0, BANK), early)
+        def quarter_pair(q, number):
+            bank = psum.tile([P, BANK], F32, name="bank_%d" % number)
+            for h in range(2):
+                a = (2 * h + q) * (S // 4)
+                one_pass(bank[:, h * (S // 4) : (h + 1) * (S // 4)], Y, 1, a, a + S // 4)
+            return lambda copy: copy(out=quarters[:, q], in_=bank[:].rearrange("p (h n) -> p h n", h=2))
+
+        for number, cuts in enumerate(pieces):
+            product(Y, 0, cuts, number)(nc.scalar.copy)
 
         picked = [keep.tile([P, U], F32, name="picked_%d" % m) for m in blocks]
         logits = [keep.tile([P, U], F32, name="logits_%d" % m) for m in blocks]
         gates = [keep.tile([P, U], F32, name="gates_%d" % m) for m in blocks]
-        for m in blocks:
-            nc.vector.tensor_copy(out=picked[m][:], in_=tables[Y][m][:].indirect(dst_t[:]))
-        for m in blocks:
-            nc.vector.tensor_tensor(logits[m][:], tables[E][m][:].indirect(src_t[:]), picked[m][:], ADD)
-            nc.scalar.activation(gates[m][:], logits[m][:], SIGMOID)
-        for m in blocks:
+        early, late = (0, BANK), (BANK, S)
+        halves = ((0, U // 2), (U // 2, U))
+        on_vector, on_scalar = nc.vector.tensor_copy, nc.scalar.copy
+
+        def pick(m, a, b):
+            nc.scalar.activation(picked[m][:, a:b], tables[Y][m][:].indirect(entries(dst_t, a, b)), COPY)
+
+        def add(m, a, b):
+            nc.vector.tensor_tensor(logits[m][:, a:b], tables[E][m][:].indirect(entries(src_t, a, b)), picked[m][:, a:b], ADD)
+
+        def gate(m, a, b):
+            nc.scalar.activation(gates[m][:, a:b], logits[m][:, a:b], SIGMOID)
+
+        def finish(m):
             for a, b in spans(STORE_CUTS[m]):
                 result = keep.tile([P, b - a], F32, name="result_%d_%d" % (m, a))
                 nc.vector.tensor_tensor(result[:], tables[H][m][:].indirect(entries(src_t, a, b)), gates[m][:, a:b], MULT)
                 nc.sync.dma_start(out=out[m * P : (m + 1) * P, a:b], in_=result[:])
+
+        pick(0, 0, U)
+        quarter_pair(0, 7)(on_vector)
+        product(E, 0, late, 5)(on_vector)
+        product(E, 0, early, 2)(on_vector)
+        product(E, 1, early, 3)(on_vector)
+        quarter_pair(1, 5)(on_vector)
+        product(E, 1, late, 4)(on_scalar)
+        add(0, 0, U)
+        for a, b in halves:
+            pick(1, a, b)
+            add(1, a, b)
+        product(H, 0, early, 2)(on_scalar)
+        product(H, 0, late, 3)(on_scalar)
+        for a, b in halves:
+            gate(0, a, b)
+        product(H, 1, early, 5)(on_scalar)
+        product(H, 1, late, 4)(on_scalar)
+        finish(0)
+        for a, b in halves:
+            gate(1, a, b)
+        finish(1)

@@ -22,15 +22,10 @@ PACK = 4
 BANK = 512
 Y, E, H = 0, 1, 2
 
-LOAD_CUTS = ((0, T), (0, 896, T), (0, 896, T), (0, 768, 1664, T))
-GPSIMD_END = 1280
-FIRST_SPLIT = 1376
-VECTOR_SHARE = 480
-MIDDLE_SHARE = 384
-ORDER = (2, 0, 1, 3)
-LAST = (VECTOR_SHARE, VECTOR_SHARE + 256)
+RUN = 256
 WINDOW = ((1376, S), (1040, S), (S, S))
-STORE_CUTS = ((0, 512, U), (0, 384, 704, 896, U))
+FIRST_CUTS = (0, 320, 576)
+HANDED = (576, 896)
 
 
 def entries(lst, a, b):
@@ -53,7 +48,6 @@ def tile_picked_edgeatt_sigmoid_e_kernel(
         src_t = keep.tile([P, U // 16], U16, name="src_t")
         dst_t = keep.tile([P, U // 16], U16, name="dst_t")
         x32 = [keep.tile([P, T], F32, name="x32_%d" % j) for j in range(PACK)]
-        x16 = [keep.tile([P, T], BF16, name="x16_%d" % j) for j in range(PACK)]
         woven = keep.tile([P, S, PACK], BF16, name="woven", tag="woven", align_bytes=64)
         x_codes = keep.tile([P, S], U32, name="x_codes", align_bytes=64)
         x_scales = keep.tile([P, S], U8, name="x_scales", align_bytes=64)
@@ -75,10 +69,9 @@ def tile_picked_edgeatt_sigmoid_e_kernel(
                 nc.sync.dma_start(out=w_scales[i][32 * q : 32 * q + 4, :].bitcast(I32), in_=rows[4 * q : 4 * q + 4, :])
 
         planes = xT.rearrange("(p j) t -> j p t", j=PACK)
-        for turn, j in enumerate(ORDER):
-            for a, b in spans(LOAD_CUTS[turn]):
-                nc.sync.dma_start(out=x32[j][:, a:b], in_=planes[j][:, a:b])
-            if turn == 0:
+        for j in range(PACK):
+            nc.sync.dma_start(out=x32[j][:], in_=planes[j])
+            if j == 0:
                 nc.sync.dma_start(offs_t[:], offs)
                 load_scales(Y)
         for i in (Y, E, H):
@@ -88,18 +81,25 @@ def tile_picked_edgeatt_sigmoid_e_kernel(
         load_scales(E)
         load_scales(H)
 
-        for turn, j in enumerate(ORDER):
-            if turn == 0:
-                nc.scalar.copy(out=x16[j][:, FIRST_SPLIT:T], in_=x32[j][:, FIRST_SPLIT:T])
-                nc.vector.tensor_copy(out=x16[j][:, 0:FIRST_SPLIT], in_=x32[j][:, 0:FIRST_SPLIT])
-            else:
-                for a, b in spans(LOAD_CUTS[turn]):
-                    engine = nc.gpsimd if b <= GPSIMD_END or (j, b) == (PACK - 1, T) else nc.vector
-                    engine.tensor_copy(out=x16[j][:, a:b], in_=x32[j][:, a:b])
-            for a, b in [(0, MIDDLE_SHARE)] if j < 2 else [(0, VECTOR_SHARE)]:
+        def gather_dense(j, a, b):
+            dense = keep.tile([P, b - a], BF16, name="dense_%d_%d" % (j, a))
+            nc.scalar.activation(dense[:], x32[j][:].indirect(entries(offs_t, a, b)), COPY)
+            return dense
+
+        for j in range(PACK):
+            for a, b in spans((0, RUN, 2 * RUN) if j == PACK - 1 else (0, 2 * RUN)):
                 nc.vector.tensor_copy(out=woven[:, a:b, j], in_=x32[j][:].indirect(entries(offs_t, a, b)))
-            for a, b in [(MIDDLE_SHARE, S)] if j < 2 else [(VECTOR_SHARE, 768), (768, S)]:
-                nc.scalar.activation(woven[:, a:b, j], x16[j][:].indirect(entries(offs_t, a, b)), COPY)
+            if j < 2:
+                nc.gpsimd.tensor_copy(out=woven[:, 2 * RUN : S, j], in_=gather_dense(j, 2 * RUN, S)[:])
+            elif j == 2:
+                own = gather_dense(j, 3 * RUN, S)
+                nc.gpsimd.tensor_copy(out=woven[:, 2 * RUN : 3 * RUN, j], in_=gather_dense(j, 2 * RUN, 3 * RUN)[:])
+                nc.scalar.copy(out=woven[:, 3 * RUN : S, j], in_=own[:])
+            else:
+                nc.gpsimd.tensor_copy(out=woven[:, 2 * RUN : 3 * RUN, j], in_=gather_dense(j, 2 * RUN, 3 * RUN)[:])
+                own = gather_dense(j, 3 * RUN, S)
+                for a, b in spans((0, RUN // 2, RUN)):
+                    nc.scalar.copy(out=woven[:, 3 * RUN + a : 3 * RUN + b, j], in_=own[:, a:b])
 
         blocks = range(N // P)
         tables = [[keep.tile([P, WINDOW[i][m]], F32, name="table_%d_%d" % (i, m)) if (i, m) != (Y, 1) else None for m in blocks] for i in (Y, E, H)]
@@ -157,11 +157,15 @@ def tile_picked_edgeatt_sigmoid_e_kernel(
         def gate(m, a, b):
             nc.scalar.activation(gates[m][:, a:b], logits[m][:, a:b], SIGMOID)
 
-        def finish(m):
-            for a, b in spans(STORE_CUTS[m]):
-                result = keep.tile([P, b - a], F32, name="result_%d_%d" % (m, a))
-                nc.vector.tensor_tensor(result[:], tables[H][m][:].indirect(entries(src_t, a, b)), gates[m][:, a:b], MULT)
-                nc.sync.dma_start(out=out[m * P : (m + 1) * P, a:b], in_=result[:])
+        def store(m, a, b, result):
+            nc.sync.dma_start(out=out[m * P : (m + 1) * P, a:b], in_=result)
+
+        def finish(m, a, b, result):
+            nc.vector.tensor_tensor(result, tables[H][m][:].indirect(entries(src_t, a, b)), gates[m][:, a:b], MULT)
+            store(m, a, b, result)
+
+        def fresh(m, a, b):
+            return keep.tile([P, b - a], F32, name="result_%d_%d" % (m, a))[:]
 
         pick(0, 0, U)
         quarter_pair(0, 7)(on_vector)
@@ -180,7 +184,17 @@ def tile_picked_edgeatt_sigmoid_e_kernel(
             gate(0, a, b)
         product(H, 1, early, 5)(on_scalar)
         product(H, 1, late, 4)(on_scalar)
-        finish(0)
         for a, b in halves:
-            gate(1, a, b)
-        finish(1)
+            finish(0, a, b, fresh(0, a, b))
+        a, b = HANDED
+        gate(1, 0, U // 2)
+        gate(1, U // 2, b)
+        for c, d in spans(FIRST_CUTS):
+            finish(1, c, d, fresh(1, c, d))
+        fetched = keep.tile([P, b - a], F32, name="fetched", tag="fetched")
+        nc.scalar.activation(fetched[:], tables[H][1][:].indirect(entries(src_t, a, b)), COPY)
+        result = fresh(1, a, b)
+        nc.vector.tensor_tensor(result, fetched[:], gates[1][:, a:b], MULT)
+        store(1, a, b, result)
+        gate(1, b, U)
+        finish(1, b, U, fresh(1, b, U))

@@ -23,6 +23,9 @@ BANK = 512
 Y, E, H = 0, 1, 2
 
 RUN = 256
+DIRECT = 2 * RUN
+SPLIT = 736
+LAST_LAID = (736, 896, S)
 WINDOW = ((1376, S), (1040, S), (S, S))
 FIRST_CUTS = (0, 320, 576)
 HANDED = (576, 896)
@@ -81,25 +84,29 @@ def tile_picked_edgeatt_sigmoid_e_kernel(
         load_scales(E)
         load_scales(H)
 
-        def gather_dense(j, a, b):
-            dense = keep.tile([P, b - a], BF16, name="dense_%d_%d" % (j, a))
-            nc.scalar.activation(dense[:], x32[j][:].indirect(entries(offs_t, a, b)), COPY)
-            return dense
+        dense = [keep.tile([P, 2, S - DIRECT], BF16, name="dense_%d" % u) for u in range(2)]
 
-        for j in range(PACK):
-            for a, b in spans((0, RUN, 2 * RUN) if j == PACK - 1 else (0, 2 * RUN)):
-                nc.vector.tensor_copy(out=woven[:, a:b, j], in_=x32[j][:].indirect(entries(offs_t, a, b)))
-            if j < 2:
-                nc.gpsimd.tensor_copy(out=woven[:, 2 * RUN : S, j], in_=gather_dense(j, 2 * RUN, S)[:])
-            elif j == 2:
-                own = gather_dense(j, 3 * RUN, S)
-                nc.gpsimd.tensor_copy(out=woven[:, 2 * RUN : 3 * RUN, j], in_=gather_dense(j, 2 * RUN, 3 * RUN)[:])
-                nc.scalar.copy(out=woven[:, 3 * RUN : S, j], in_=own[:])
-            else:
-                nc.gpsimd.tensor_copy(out=woven[:, 2 * RUN : 3 * RUN, j], in_=gather_dense(j, 2 * RUN, 3 * RUN)[:])
-                own = gather_dense(j, 3 * RUN, S)
-                for a, b in spans((0, RUN // 2, RUN)):
-                    nc.scalar.copy(out=woven[:, 3 * RUN + a : 3 * RUN + b, j], in_=own[:, a:b])
+        def gather_dense(j, a, b):
+            target = dense[j // 2][:, j % 2, a - DIRECT : b - DIRECT]
+            nc.scalar.activation(target, x32[j][:].indirect(entries(offs_t, a, b)), COPY)
+
+        def lay(copy, u, a, b):
+            pair = dense[u][:, :, a - DIRECT : b - DIRECT].rearrange("p j n -> p n j")
+            copy(out=woven[:, a:b, 2 * u : 2 * u + 2], in_=pair)
+
+        for j in range(PACK - 1):
+            nc.vector.tensor_copy(out=woven[:, 0:DIRECT, j], in_=x32[j][:].indirect(entries(offs_t, 0, DIRECT)))
+            gather_dense(j, DIRECT, S)
+            if j == 1:
+                lay(nc.gpsimd.tensor_copy, 0, DIRECT, S)
+        j = PACK - 1
+        for a, b in spans((0, RUN, DIRECT)):
+            nc.vector.tensor_copy(out=woven[:, a:b, j], in_=x32[j][:].indirect(entries(offs_t, a, b)))
+        gather_dense(j, DIRECT, SPLIT)
+        lay(nc.gpsimd.tensor_copy, 1, DIRECT, SPLIT)
+        gather_dense(j, SPLIT, S)
+        for a, b in spans(LAST_LAID):
+            lay(nc.scalar.copy, 1, a, b)
 
         blocks = range(N // P)
         tables = [[keep.tile([P, WINDOW[i][m]], F32, name="table_%d_%d" % (i, m)) if (i, m) != (Y, 1) else None for m in blocks] for i in (Y, E, H)]

@@ -25,10 +25,9 @@ Y, E, H = 0, 1, 2
 RUN = 256
 DIRECT = 2 * RUN
 SPLIT = 736
-LAST_LAID = (736, 896, S)
-WINDOW = ((1376, S), (1040, S), (S, S))
-FIRST_CUTS = (0, 320, 576)
-HANDED = (576, 896)
+PIECES = (0, 256, 512, 768, 896, S)
+HALVES = (0, U // 2, U)
+HANDED = (512, 896)
 
 
 def entries(lst, a, b):
@@ -36,7 +35,7 @@ def entries(lst, a, b):
 
 
 def spans(cuts):
-    return zip(cuts, cuts[1:])
+    return list(zip(cuts, cuts[1:]))
 
 
 def tile_picked_edgeatt_sigmoid_e_kernel(
@@ -66,50 +65,95 @@ def tile_picked_edgeatt_sigmoid_e_kernel(
         nc.vector.memset(warm[:, 0:1], 0.0)
         nc.scalar.activation(warm[:, 1:2], warm[:, 0:1], SIGMOID)
 
-        def load_scales(i):
+        def load_scales(i, queue):
             rows = scales_in[i][0].bitcast(I32)
             for q in range(4):
-                nc.sync.dma_start(out=w_scales[i][32 * q : 32 * q + 4, :].bitcast(I32), in_=rows[4 * q : 4 * q + 4, :])
+                queue.dma_start(out=w_scales[i][32 * q : 32 * q + 4, :].bitcast(I32), in_=rows[4 * q : 4 * q + 4, :])
 
+        def load_codes(i):
+            nc.sync.dma_start(out=w_codes[i][:], in_=words_in[i][0].rearrange("p n t -> p (n t)").bitcast(I32))
+
+        load_scales(Y, nc.gpsimd)
         planes = xT.rearrange("(p j) t -> j p t", j=PACK)
         for j in range(PACK):
             nc.sync.dma_start(out=x32[j][:], in_=planes[j])
             if j == 0:
                 nc.sync.dma_start(offs_t[:], offs)
-                load_scales(Y)
-        for i in (Y, E, H):
-            nc.sync.dma_start(out=w_codes[i][:], in_=words_in[i][0].rearrange("p n t -> p (n t)").bitcast(I32))
+        load_codes(Y)
         nc.sync.dma_start(dst_t[:], dst)
+        load_codes(E)
+        load_scales(E, nc.sync)
+        load_codes(H)
+        load_scales(H, nc.sync)
         nc.sync.dma_start(src_t[:], src)
-        load_scales(E)
-        load_scales(H)
 
-        dense = [keep.tile([P, 2, S - DIRECT], BF16, name="dense_%d" % u) for u in range(2)]
+        dense = keep.tile([P, PACK, S - DIRECT], BF16, name="dense", align_bytes=64)
+
+        def gather_direct(j, a, b):
+            nc.vector.tensor_copy(out=woven[:, a:b, j], in_=x32[j][:].indirect(entries(offs_t, a, b)))
 
         def gather_dense(j, a, b):
-            target = dense[j // 2][:, j % 2, a - DIRECT : b - DIRECT]
+            target = dense[:, j, a - DIRECT : b - DIRECT]
             nc.scalar.activation(target, x32[j][:].indirect(entries(offs_t, a, b)), COPY)
 
         def lay(copy, u, a, b):
-            pair = dense[u][:, :, a - DIRECT : b - DIRECT].rearrange("p j n -> p n j")
+            pair = dense[:, 2 * u : 2 * u + 2, a - DIRECT : b - DIRECT].rearrange("p j n -> p n j")
             copy(out=woven[:, a:b, 2 * u : 2 * u + 2], in_=pair)
 
+        idle_codes = keep.tile([P, BANK], U32, name="idle_codes", align_bytes=64)
+        idle_scales = keep.tile([P, BANK], U8, name="idle_scales", align_bytes=64)
+
+        def quantise_idle(a, count):
+            b = a + count * (S - DIRECT) // PACK
+            rows = dense[:, 0:count, :].rearrange("p j n -> p (j n)")
+            nc.vector.quantize_mx(out=idle_codes[:, a:b].bitcast(FP8X4), scales=idle_scales[:, a:b], in_=rows)
+
         for j in range(PACK - 1):
-            nc.vector.tensor_copy(out=woven[:, 0:DIRECT, j], in_=x32[j][:].indirect(entries(offs_t, 0, DIRECT)))
+            gather_direct(j, 0, DIRECT)
             gather_dense(j, DIRECT, S)
+            if j == 0:
+                quantise_idle(384, 1)
             if j == 1:
                 lay(nc.gpsimd.tensor_copy, 0, DIRECT, S)
-        j = PACK - 1
+        quantise_idle(0, 3)
+        idle = psum.tile([P, BANK], F32, name="bank_7")
+        for turn in range(4):
+            nc.tensor.matmul_mx(
+                out=idle[0:32, :],
+                lhsT=idle_codes[:, 0:32].bitcast(FP8X4),
+                lhsT_scale=idle_scales[:, 0:32],
+                rhs=idle_codes[:].bitcast(FP8X4),
+                rhs_scale=idle_scales[:],
+                start=True,
+                stop=True,
+            )
+        last = PACK - 1
         for a, b in spans((0, RUN, DIRECT)):
-            nc.vector.tensor_copy(out=woven[:, a:b, j], in_=x32[j][:].indirect(entries(offs_t, a, b)))
-        gather_dense(j, DIRECT, SPLIT)
+            gather_direct(last, a, b)
+        gather_dense(last, DIRECT, SPLIT)
         lay(nc.gpsimd.tensor_copy, 1, DIRECT, SPLIT)
-        gather_dense(j, SPLIT, S)
-        for a, b in spans(LAST_LAID):
+        gather_dense(last, SPLIT, S)
+        for a, b in spans((SPLIT, PIECES[-2], S)):
             lay(nc.scalar.copy, 1, a, b)
+        for a, b in spans(PIECES):
+            nc.vector.quantize_mx(
+                out=x_codes[:, a:b].bitcast(FP8X4),
+                scales=x_scales[:, a:b],
+                in_=woven[:, a:b, :].rearrange("p n j -> p (n j)"),
+            )
 
         blocks = range(N // P)
-        tables = [[keep.tile([P, WINDOW[i][m]], F32, name="table_%d_%d" % (i, m)) if (i, m) != (Y, 1) else None for m in blocks] for i in (Y, E, H)]
+        tables = [
+            [keep.tile([P, S], F32, name="table_%d_%d" % (i, m), tag="woven" if (i, m) == (Y, 1) else "table_%d_%d" % (i, m), align_bytes=64) for m in blocks]
+            for i in (Y, E, H)
+        ]
+        picked = [keep.tile([P, U], F32, name="picked_%d" % m) for m in blocks]
+        logits = [keep.tile([P, U], F32, name="logits_%d" % m) for m in blocks]
+        gates = [keep.tile([P, U], F32, name="gates_%d" % m) for m in blocks]
+        on_vector, on_scalar = nc.vector.tensor_copy, nc.scalar.copy
+
+        def bank(number):
+            return psum.tile([P, BANK], F32, name="bank_%d" % number)
 
         def one_pass(target, i, m, a, b):
             nc.tensor.matmul_mx(
@@ -122,38 +166,10 @@ def tile_picked_edgeatt_sigmoid_e_kernel(
                 stop=True,
             )
 
-        def product(i, m, cuts, number):
-            a, b = cuts
-            bank = psum.tile([P, BANK], F32, name="bank_%d" % number)
-            one_pass(bank[:, 0 : b - a], i, m, a, b)
-            return lambda copy: copy(out=tables[i][m][:, a:b], in_=bank[:, 0 : b - a])
-
-        pieces = ((0, 256), (256, 512), (512, 768), (768, 896), (896, S))
-        for a, b in pieces:
-            nc.vector.quantize_mx(
-                out=x_codes[:, a:b].bitcast(FP8X4),
-                scales=x_scales[:, a:b],
-                in_=woven[:, a:b, :].rearrange("p n j -> p (n j)"),
-            )
-        tables[Y][1] = keep.tile([P, S], F32, name="table_y1", tag="woven", align_bytes=64)
-        quarters = tables[Y][1][:].rearrange("p (h q n) -> p q h n", h=2, q=2)
-
-        def quarter_pair(q, number):
-            bank = psum.tile([P, BANK], F32, name="bank_%d" % number)
-            for h in range(2):
-                a = (2 * h + q) * (S // 4)
-                one_pass(bank[:, h * (S // 4) : (h + 1) * (S // 4)], Y, 1, a, a + S // 4)
-            return lambda copy: copy(out=quarters[:, q], in_=bank[:].rearrange("p (h n) -> p h n", h=2))
-
-        for number, cuts in enumerate(pieces):
-            product(Y, 0, cuts, number)(nc.scalar.copy)
-
-        picked = [keep.tile([P, U], F32, name="picked_%d" % m) for m in blocks]
-        logits = [keep.tile([P, U], F32, name="logits_%d" % m) for m in blocks]
-        gates = [keep.tile([P, U], F32, name="gates_%d" % m) for m in blocks]
-        early, late = (0, BANK), (BANK, S)
-        halves = ((0, U // 2), (U // 2, U))
-        on_vector, on_scalar = nc.vector.tensor_copy, nc.scalar.copy
+        def product(i, m, a, b, number, copy):
+            target = bank(number)[:, 0 : b - a]
+            one_pass(target, i, m, a, b)
+            copy(out=tables[i][m][:, a:b], in_=target)
 
         def pick(m, a, b):
             nc.scalar.activation(picked[m][:, a:b], tables[Y][m][:].indirect(entries(dst_t, a, b)), COPY)
@@ -167,41 +183,54 @@ def tile_picked_edgeatt_sigmoid_e_kernel(
         def store(m, a, b, result):
             nc.sync.dma_start(out=out[m * P : (m + 1) * P, a:b], in_=result)
 
-        def finish(m, a, b, result):
+        def fresh(name, a, b):
+            return keep.tile([P, b - a], F32, name="%s_%d" % (name, a))[:]
+
+        def finish(m, a, b):
+            result = fresh("result_%d" % m, a, b)
             nc.vector.tensor_tensor(result, tables[H][m][:].indirect(entries(src_t, a, b)), gates[m][:, a:b], MULT)
             store(m, a, b, result)
 
-        def fresh(m, a, b):
-            return keep.tile([P, b - a], F32, name="result_%d_%d" % (m, a))[:]
+        def fetch(m, a, b):
+            fetched = fresh("fetched", a, b)
+            nc.scalar.activation(fetched, tables[H][m][:].indirect(entries(src_t, a, b)), COPY)
+            return fetched
 
-        pick(0, 0, U)
-        quarter_pair(0, 7)(on_vector)
-        product(E, 0, late, 5)(on_vector)
-        product(E, 0, early, 2)(on_vector)
-        product(E, 1, early, 3)(on_vector)
-        quarter_pair(1, 5)(on_vector)
-        product(E, 1, late, 4)(on_scalar)
-        add(0, 0, U)
-        for a, b in halves:
-            pick(1, a, b)
-            add(1, a, b)
-        product(H, 0, early, 2)(on_scalar)
-        product(H, 0, late, 3)(on_scalar)
-        for a, b in halves:
+        def finish_plainly(m, a, b, fetched):
+            result = fresh("result_%d" % m, a, b)
+            nc.vector.tensor_tensor(result, fetched, gates[m][:, a:b], MULT)
+            store(m, a, b, result)
+
+        early = bank(5)
+        for number, (a, b) in enumerate(spans(PIECES)):
+            product(Y, 0, a, b, number, on_vector if a == BANK else on_scalar)
+            if b <= BANK:
+                one_pass(early[:, a:b], Y, 1, a, b)
+        on_vector(out=tables[Y][1][:, 0:BANK], in_=early[:])
+        product(Y, 1, BANK, S, 7, on_scalar)
+        product(E, 0, 0, BANK, 6, on_vector)
+        product(E, 0, BANK, S, 0, on_vector)
+        product(E, 1, 0, BANK, 1, on_vector)
+        product(E, 1, BANK, S, 2, on_vector)
+        for m in blocks:
+            for a, b in spans(HALVES):
+                pick(m, a, b)
+                add(m, a, b)
+        product(H, 0, 0, BANK, 0, on_scalar)
+        product(H, 0, BANK, S, 1, on_scalar)
+        for a, b in spans(HALVES):
             gate(0, a, b)
-        product(H, 1, early, 5)(on_scalar)
-        product(H, 1, late, 4)(on_scalar)
-        for a, b in halves:
-            finish(0, a, b, fresh(0, a, b))
+            finish(0, a, b)
+        product(H, 1, 0, BANK, 2, on_scalar)
+        product(H, 1, BANK, S, 0, on_scalar)
         a, b = HANDED
-        gate(1, 0, U // 2)
-        gate(1, U // 2, b)
-        for c, d in spans(FIRST_CUTS):
-            finish(1, c, d, fresh(1, c, d))
-        fetched = keep.tile([P, b - a], F32, name="fetched", tag="fetched")
-        nc.scalar.activation(fetched[:], tables[H][1][:].indirect(entries(src_t, a, b)), COPY)
-        result = fresh(1, a, b)
-        nc.vector.tensor_tensor(result, fetched[:], gates[1][:, a:b], MULT)
-        store(1, a, b, result)
+        gate(1, 0, a)
+        gate(1, a, b)
+        middle = (a + b) // 2
+        parts = [(c, d, fetch(1, c, d)) for c, d in spans((a, middle, b))]
         gate(1, b, U)
-        finish(1, b, U, fresh(1, b, U))
+        finish(1, 0, 256)
+        finish(1, 256, a)
+        for c, d, fetched in parts:
+            finish_plainly(1, c, d, fetched)
+        finish(1, b, U)

@@ -73,12 +73,12 @@ def tile_picked_edgeatt_sigmoid_e_kernel(
         def load_codes(i):
             nc.sync.dma_start(out=w_codes[i][:], in_=words_in[i][0].rearrange("p n t -> p (n t)").bitcast(I32))
 
-        load_scales(Y, nc.gpsimd)
         planes = xT.rearrange("(p j) t -> j p t", j=PACK)
         for j in range(PACK):
             nc.sync.dma_start(out=x32[j][:], in_=planes[j])
             if j == 0:
                 nc.sync.dma_start(offs_t[:], offs)
+        load_scales(Y, nc.sync)
         load_codes(Y)
         nc.sync.dma_start(dst_t[:], dst)
         load_codes(E)

@@ -24,10 +24,10 @@ Y, E, H = 0, 1, 2
 
 RUN = 256
 DIRECT = 2 * RUN
-SPLIT = 736
+SPLIT = 672
 PIECES = (0, 256, 512, 768, 896, S)
 HALVES = (0, U // 2, U)
-HANDED = (512, 896)
+LAST_CUTS = (0, 256, 512, 704, 896, U)
 
 
 def entries(lst, a, b):
@@ -80,9 +80,9 @@ def tile_picked_edgeatt_sigmoid_e_kernel(
                 nc.sync.dma_start(offs_t[:], offs)
         load_scales(Y, nc.sync)
         load_codes(Y)
-        nc.sync.dma_start(dst_t[:], dst)
         load_codes(E)
         load_scales(E, nc.sync)
+        nc.sync.dma_start(dst_t[:], dst)
         load_codes(H)
         load_scales(H, nc.sync)
         nc.sync.dma_start(src_t[:], src)
@@ -132,7 +132,8 @@ def tile_picked_edgeatt_sigmoid_e_kernel(
             gather_direct(last, a, b)
         gather_dense(last, DIRECT, SPLIT)
         lay(nc.gpsimd.tensor_copy, 1, DIRECT, SPLIT)
-        gather_dense(last, SPLIT, S)
+        for a, b in spans((SPLIT, PIECES[-2], S)):
+            gather_dense(last, a, b)
         for a, b in spans((SPLIT, PIECES[-2], S)):
             lay(nc.scalar.copy, 1, a, b)
         for a, b in spans(PIECES):
@@ -201,36 +202,35 @@ def tile_picked_edgeatt_sigmoid_e_kernel(
             nc.vector.tensor_tensor(result, fetched, gates[m][:, a:b], MULT)
             store(m, a, b, result)
 
-        early = bank(5)
+        second = [bank(5), bank(7)]
         for number, (a, b) in enumerate(spans(PIECES)):
-            product(Y, 0, a, b, number, on_vector if a == BANK else on_scalar)
-            if b <= BANK:
-                one_pass(early[:, a:b], Y, 1, a, b)
-        on_vector(out=tables[Y][1][:, 0:BANK], in_=early[:])
-        product(Y, 1, BANK, S, 7, on_scalar)
-        product(E, 0, 0, BANK, 6, on_vector)
+            product(Y, 0, a, b, number, on_scalar)
+            if b % RUN == 0:
+                one_pass(second[a // BANK][:, (b - RUN) % BANK : (b - RUN) % BANK + RUN], Y, 1, b - RUN, b)
+        for half, (a, b) in enumerate(spans(HALVES)):
+            on_vector(out=tables[Y][1][:, a:b], in_=second[half][:])
+        product(E, 0, 0, BANK, 6, on_scalar)
         product(E, 0, BANK, S, 0, on_vector)
         product(E, 1, 0, BANK, 1, on_vector)
         product(E, 1, BANK, S, 2, on_vector)
+        product(H, 0, 0, RUN, 3, on_vector)
         for m in blocks:
             for a, b in spans(HALVES):
                 pick(m, a, b)
                 add(m, a, b)
-        product(H, 0, 0, BANK, 0, on_scalar)
+        product(H, 0, RUN, BANK, 0, on_scalar)
         product(H, 0, BANK, S, 1, on_scalar)
         for a, b in spans(HALVES):
             gate(0, a, b)
             finish(0, a, b)
         product(H, 1, 0, BANK, 2, on_scalar)
         product(H, 1, BANK, S, 0, on_scalar)
-        a, b = HANDED
-        gate(1, 0, a)
-        gate(1, a, b)
-        middle = (a + b) // 2
-        parts = [(c, d, fetch(1, c, d)) for c, d in spans((a, middle, b))]
-        gate(1, b, U)
-        finish(1, 0, 256)
-        finish(1, 256, a)
-        for c, d, fetched in parts:
+        parts = spans(LAST_CUTS)
+        for (a, b), (c, d) in zip(parts[0::2], parts[1::2]):
+            gate(1, a, d)
+            fetched = fetch(1, c, d)
+            finish(1, a, b)
             finish_plainly(1, c, d, fetched)
-        finish(1, b, U)
+        a, b = parts[-1]
+        gate(1, a, b)
+        finish(1, a, b)

@@ -103,25 +103,27 @@ def tile_picked_edgeatt_sigmoid_e_kernel(
         idle_codes = keep.tile([P, BANK], U32, name="idle_codes", align_bytes=64)
         idle_scales = keep.tile([P, BANK], U8, name="idle_scales", align_bytes=64)
 
-        def quantise_idle(a, count):
-            b = a + count * (S - DIRECT) // PACK
-            rows = dense[:, 0:count, :].rearrange("p j n -> p (j n)")
-            nc.vector.quantize_mx(out=idle_codes[:, a:b].bitcast(FP8X4), scales=idle_scales[:, a:b], in_=rows)
+        def quantise_idle():
+            width = (S - DIRECT) // PACK
+            for a in range(0, BANK, width):
+                nc.vector.quantize_mx(out=idle_codes[:, a : a + width].bitcast(FP8X4), scales=idle_scales[:, a : a + width], in_=dense[:, 0, :])
 
         for j in range(PACK - 1):
             gather_direct(j, 0, DIRECT)
             gather_dense(j, DIRECT, S)
             if j == 0:
-                quantise_idle(384, 1)
+                quantise_idle()
             if j == 1:
                 lay(nc.gpsimd.tensor_copy, 0, DIRECT, S)
-        quantise_idle(0, 3)
+        thin_codes = keep.tile([P, 32], U32, name="thin_codes", align_bytes=64)
+        thin_scales = keep.tile([P, 32], U8, name="thin_scales", align_bytes=64)
+        nc.vector.quantize_mx(out=thin_codes[:].bitcast(FP8X4), scales=thin_scales[:], in_=dense[:, 2, 0:128])
         idle = psum.tile([P, BANK], F32, name="bank_7")
         for turn in range(4):
             nc.tensor.matmul_mx(
                 out=idle[0:32, :],
-                lhsT=idle_codes[:, 0:32].bitcast(FP8X4),
-                lhsT_scale=idle_scales[:, 0:32],
+                lhsT=thin_codes[:].bitcast(FP8X4),
+                lhsT_scale=thin_scales[:],
                 rhs=idle_codes[:].bitcast(FP8X4),
                 rhs_scale=idle_scales[:],
                 start=True,
@@ -213,12 +215,11 @@ def tile_picked_edgeatt_sigmoid_e_kernel(
         product(E, 0, BANK, S, 0, on_vector)
         product(E, 1, 0, BANK, 1, on_vector)
         product(E, 1, BANK, S, 2, on_vector)
-        product(H, 0, 0, RUN, 3, on_vector)
         for m in blocks:
             for a, b in spans(HALVES):
                 pick(m, a, b)
                 add(m, a, b)
-        product(H, 0, RUN, BANK, 0, on_scalar)
+        product(H, 0, 0, BANK, 0, on_scalar)
         product(H, 0, BANK, S, 1, on_scalar)
         for a, b in spans(HALVES):
             gate(0, a, b)

@@ -103,27 +103,25 @@ def tile_picked_edgeatt_sigmoid_e_kernel(
         idle_codes = keep.tile([P, BANK], U32, name="idle_codes", align_bytes=64)
         idle_scales = keep.tile([P, BANK], U8, name="idle_scales", align_bytes=64)
 
-        def quantise_idle():
-            width = (S - DIRECT) // PACK
-            for a in range(0, BANK, width):
-                nc.vector.quantize_mx(out=idle_codes[:, a : a + width].bitcast(FP8X4), scales=idle_scales[:, a : a + width], in_=dense[:, 0, :])
+        def quantise_idle(a, count):
+            b = a + count * (S - DIRECT) // PACK
+            rows = dense[:, 0:count, :].rearrange("p j n -> p (j n)")
+            nc.vector.quantize_mx(out=idle_codes[:, a:b].bitcast(FP8X4), scales=idle_scales[:, a:b], in_=rows)
 
         for j in range(PACK - 1):
             gather_direct(j, 0, DIRECT)
             gather_dense(j, DIRECT, S)
             if j == 0:
-                quantise_idle()
+                quantise_idle(384, 1)
             if j == 1:
                 lay(nc.gpsimd.tensor_copy, 0, DIRECT, S)
-        thin_codes = keep.tile([P, 32], U32, name="thin_codes", align_bytes=64)
-        thin_scales = keep.tile([P, 32], U8, name="thin_scales", align_bytes=64)
-        nc.vector.quantize_mx(out=thin_codes[:].bitcast(FP8X4), scales=thin_scales[:], in_=dense[:, 2, 0:128])
+        quantise_idle(0, 3)
         idle = psum.tile([P, BANK], F32, name="bank_7")
         for turn in range(4):
             nc.tensor.matmul_mx(
                 out=idle[0:32, :],
-                lhsT=thin_codes[:].bitcast(FP8X4),
-                lhsT_scale=thin_scales[:],
+                lhsT=idle_codes[:, 0:32].bitcast(FP8X4),
+                lhsT_scale=idle_scales[:, 0:32],
                 rhs=idle_codes[:].bitcast(FP8X4),
                 rhs_scale=idle_scales[:],
                 start=True,

@@ -24,7 +24,7 @@ Y, E, H = 0, 1, 2
 
 RUN = 256
 DIRECT = 2 * RUN
-SPLIT = 672
+SPLIT = 736
 PIECES = (0, 256, 512, 768, 896, S)
 HALVES = (0, U // 2, U)
 LAST_CUTS = (0, 256, 512, 704, 896, U)

@@ -23,11 +23,10 @@ BANK = 512
 Y, E, H = 0, 1, 2
 
 RUN = 256
-DIRECT = 2 * RUN
-SPLIT = 736
-PIECES = (0, 256, 512, 768, 896, S)
-HALVES = (0, U // 2, U)
-LAST_CUTS = (0, 256, 512, 704, 896, U)
+ORDER = (2, 0, 1, 3)
+EVEN = S // 2
+MID = (288, 704)
+THIN = 32
 
 
 def entries(lst, a, b):
@@ -50,107 +49,89 @@ def tile_picked_edgeatt_sigmoid_e_kernel(
         src_t = keep.tile([P, U // 16], U16, name="src_t")
         dst_t = keep.tile([P, U // 16], U16, name="dst_t")
         x32 = [keep.tile([P, T], F32, name="x32_%d" % j) for j in range(PACK)]
-        woven = keep.tile([P, S, PACK], BF16, name="woven", tag="woven", align_bytes=64)
+        woven = keep.tile([P, S, PACK], BF16, name="woven", align_bytes=64)
         x_codes = keep.tile([P, S], U32, name="x_codes", align_bytes=64)
         x_scales = keep.tile([P, S], U8, name="x_scales", align_bytes=64)
         w_codes = [keep.tile([P, N], I32, name="w_codes_%d" % i, align_bytes=64) for i in (Y, E, H)]
-        w_scales = [keep.tile([P, N], U8, name="w_scales_%d" % i, align_bytes=64) for i in (Y, E, H)]
+        w_scales = keep.tile([P, 3 * N], U8, name="w_scales", align_bytes=64)
         words_in = (w1_words, w2_words, w3_words)
         scales_in = (w1_scales, w2_scales, w3_scales)
 
-        for i in (Y, E, H):
-            nc.vector.memset(w_scales[i][:].bitcast(I32), 0)
+        nc.vector.memset(w_scales[:].bitcast(I32), 0)
 
         warm = keep.tile([P, 2], F32, name="warm")
         nc.vector.memset(warm[:, 0:1], 0.0)
         nc.scalar.activation(warm[:, 1:2], warm[:, 0:1], SIGMOID)
 
-        def load_scales(i, queue):
+        def load_scales(i):
             rows = scales_in[i][0].bitcast(I32)
             for q in range(4):
-                queue.dma_start(out=w_scales[i][32 * q : 32 * q + 4, :].bitcast(I32), in_=rows[4 * q : 4 * q + 4, :])
+                target = w_scales[32 * q : 32 * q + 4, i * N : (i + 1) * N]
+                nc.sync.dma_start(out=target.bitcast(I32), in_=rows[4 * q : 4 * q + 4, :])
 
-        def load_codes(i):
-            nc.sync.dma_start(out=w_codes[i][:], in_=words_in[i][0].rearrange("p n t -> p (n t)").bitcast(I32))
+        def load_codes(i, a, b):
+            words = words_in[i][0].rearrange("p n t -> p (n t)").bitcast(I32)
+            nc.sync.dma_start(out=w_codes[i][:, a:b], in_=words[:, a:b])
 
         planes = xT.rearrange("(p j) t -> j p t", j=PACK)
-        for j in range(PACK):
-            nc.sync.dma_start(out=x32[j][:], in_=planes[j])
-            if j == 0:
-                nc.sync.dma_start(offs_t[:], offs)
-        load_scales(Y, nc.sync)
-        load_codes(Y)
-        load_codes(E)
-        load_scales(E, nc.sync)
+
+        def load_plane(turn):
+            nc.sync.dma_start(out=x32[ORDER[turn]][:], in_=planes[ORDER[turn]])
+
+        load_plane(0)
+        nc.sync.dma_start(offs_t[:], offs)
+        load_codes(Y, 0, THIN)
+        load_scales(E)
+        load_plane(1)
+        load_scales(H)
+        load_plane(2)
+        load_scales(Y)
+        load_plane(3)
+        load_codes(Y, THIN, N)
+        load_codes(E, 0, N)
+        load_codes(H, 0, N)
         nc.sync.dma_start(dst_t[:], dst)
-        load_codes(H)
-        load_scales(H, nc.sync)
         nc.sync.dma_start(src_t[:], src)
 
-        dense = keep.tile([P, PACK, S - DIRECT], BF16, name="dense", align_bytes=64)
-
-        def gather_direct(j, a, b):
-            nc.vector.tensor_copy(out=woven[:, a:b, j], in_=x32[j][:].indirect(entries(offs_t, a, b)))
-
-        def gather_dense(j, a, b):
-            target = dense[:, j, a - DIRECT : b - DIRECT]
-            nc.scalar.activation(target, x32[j][:].indirect(entries(offs_t, a, b)), COPY)
-
-        def lay(copy, u, a, b):
-            pair = dense[:, 2 * u : 2 * u + 2, a - DIRECT : b - DIRECT].rearrange("p j n -> p n j")
-            copy(out=woven[:, a:b, 2 * u : 2 * u + 2], in_=pair)
-
-        idle_codes = keep.tile([P, BANK], U32, name="idle_codes", align_bytes=64)
-        idle_scales = keep.tile([P, BANK], U8, name="idle_scales", align_bytes=64)
-
-        def quantise_idle(a, count):
-            b = a + count * (S - DIRECT) // PACK
-            rows = dense[:, 0:count, :].rearrange("p j n -> p (j n)")
-            nc.vector.quantize_mx(out=idle_codes[:, a:b].bitcast(FP8X4), scales=idle_scales[:, a:b], in_=rows)
-
-        for j in range(PACK - 1):
-            gather_direct(j, 0, DIRECT)
-            gather_dense(j, DIRECT, S)
-            if j == 0:
-                quantise_idle(384, 1)
-            if j == 1:
-                lay(nc.gpsimd.tensor_copy, 0, DIRECT, S)
-        quantise_idle(0, 3)
+        idle_codes = keep.tile([P, BANK // THIN, THIN], I32, name="idle_codes", align_bytes=64)
+        nc.gpsimd.tensor_copy(out=idle_codes[:], in_=w_codes[Y][:, 0:THIN].unsqueeze(1).to_broadcast([P, BANK // THIN, THIN]))
         idle = psum.tile([P, BANK], F32, name="bank_7")
         for turn in range(4):
             nc.tensor.matmul_mx(
-                out=idle[0:32, :],
-                lhsT=idle_codes[:, 0:32].bitcast(FP8X4),
-                lhsT_scale=idle_scales[:, 0:32],
-                rhs=idle_codes[:].bitcast(FP8X4),
-                rhs_scale=idle_scales[:],
+                out=idle[0:THIN, :],
+                lhsT=w_codes[Y][:, 0:THIN].bitcast(FP8X4),
+                lhsT_scale=w_scales[:, 0:THIN],
+                rhs=idle_codes[:].rearrange("p a b -> p (a b)").bitcast(FP8X4),
+                rhs_scale=w_scales[:, 0:BANK],
                 start=True,
                 stop=True,
             )
-        last = PACK - 1
-        for a, b in spans((0, RUN, DIRECT)):
-            gather_direct(last, a, b)
-        gather_dense(last, DIRECT, SPLIT)
-        lay(nc.gpsimd.tensor_copy, 1, DIRECT, SPLIT)
-        for a, b in spans((SPLIT, PIECES[-2], S)):
-            gather_dense(last, a, b)
-        for a, b in spans((SPLIT, PIECES[-2], S)):
-            lay(nc.scalar.copy, 1, a, b)
-        for a, b in spans(PIECES):
+
+        def weave_vector(j, a, b):
+            nc.vector.tensor_copy(out=woven[:, a:b, j], in_=x32[j][:].indirect(entries(offs_t, a, b)))
+
+        def weave_scalar(j, a, b):
+            nc.scalar.activation(woven[:, a:b, j], x32[j][:].indirect(entries(offs_t, a, b)), COPY)
+
+        for j in ORDER:
+            if j < 2:
+                weave_vector(j, 0, EVEN)
+                weave_scalar(j, EVEN, S)
+            else:
+                weave_vector(j, *MID)
+                weave_scalar(j, 0, MID[0])
+                for a, b in spans((MID[1], S - RUN, S) if j == ORDER[-1] else (MID[1], S)):
+                    weave_scalar(j, a, b)
+        for a in range(0, S, RUN):
             nc.vector.quantize_mx(
-                out=x_codes[:, a:b].bitcast(FP8X4),
-                scales=x_scales[:, a:b],
-                in_=woven[:, a:b, :].rearrange("p n j -> p (n j)"),
+                out=x_codes[:, a : a + RUN].bitcast(FP8X4),
+                scales=x_scales[:, a : a + RUN],
+                in_=woven[:, a : a + RUN, :].rearrange("p n j -> p (n j)"),
             )
 
-        blocks = range(N // P)
-        tables = [
-            [keep.tile([P, S], F32, name="table_%d_%d" % (i, m), tag="woven" if (i, m) == (Y, 1) else "table_%d_%d" % (i, m), align_bytes=64) for m in blocks]
-            for i in (Y, E, H)
-        ]
-        picked = [keep.tile([P, U], F32, name="picked_%d" % m) for m in blocks]
-        logits = [keep.tile([P, U], F32, name="logits_%d" % m) for m in blocks]
-        gates = [keep.tile([P, U], F32, name="gates_%d" % m) for m in blocks]
+        def table(i, m, tag=""):
+            return keep.tile([P, S], F32, name="table_%d_%d" % (i, m), tag=tag)
+
         on_vector, on_scalar = nc.vector.tensor_copy, nc.scalar.copy
 
         def bank(number):
@@ -160,76 +141,90 @@ def tile_picked_edgeatt_sigmoid_e_kernel(
             nc.tensor.matmul_mx(
                 out=target,
                 lhsT=w_codes[i][:, m * P : (m + 1) * P].bitcast(FP8X4),
-                lhsT_scale=w_scales[i][:, m * P : (m + 1) * P],
+                lhsT_scale=w_scales[:, i * N + m * P : i * N + (m + 1) * P],
                 rhs=x_codes[:, a:b].bitcast(FP8X4),
                 rhs_scale=x_scales[:, a:b],
                 start=True,
                 stop=True,
             )
 
-        def product(i, m, a, b, number, copy):
+        def product(i, m, a, b, number):
             target = bank(number)[:, 0 : b - a]
             one_pass(target, i, m, a, b)
-            copy(out=tables[i][m][:, a:b], in_=target)
+            return target
 
-        def pick(m, a, b):
-            nc.scalar.activation(picked[m][:, a:b], tables[Y][m][:].indirect(entries(dst_t, a, b)), COPY)
+        def fresh(name, a, b, tag=""):
+            return keep.tile([P, b - a], F32, name="%s_%d" % (name, a), tag=tag)[:]
 
-        def add(m, a, b):
-            nc.vector.tensor_tensor(logits[m][:, a:b], tables[E][m][:].indirect(entries(src_t, a, b)), picked[m][:, a:b], ADD)
+        def pick(target, y, a, b):
+            nc.scalar.activation(target, y[:].indirect(entries(dst_t, a, b)), COPY)
 
-        def gate(m, a, b):
-            nc.scalar.activation(gates[m][:, a:b], logits[m][:, a:b], SIGMOID)
+        def add(target, e, picked, a, b):
+            nc.vector.tensor_tensor(target, e[:].indirect(entries(src_t, a, b)), picked, ADD)
+
+        def gate(target, logits):
+            nc.scalar.activation(target, logits, SIGMOID)
 
         def store(m, a, b, result):
             nc.sync.dma_start(out=out[m * P : (m + 1) * P, a:b], in_=result)
 
-        def fresh(name, a, b):
-            return keep.tile([P, b - a], F32, name="%s_%d" % (name, a))[:]
-
-        def finish(m, a, b):
+        def finish(m, h, gates, a, b):
             result = fresh("result_%d" % m, a, b)
-            nc.vector.tensor_tensor(result, tables[H][m][:].indirect(entries(src_t, a, b)), gates[m][:, a:b], MULT)
+            nc.vector.tensor_tensor(result, h[:].indirect(entries(src_t, a, b)), gates[:, a:b], MULT)
             store(m, a, b, result)
 
-        def fetch(m, a, b):
-            fetched = fresh("fetched", a, b)
-            nc.scalar.activation(fetched, tables[H][m][:].indirect(entries(src_t, a, b)), COPY)
-            return fetched
+        def fetch(target, h, a, b):
+            nc.scalar.activation(target, h[:].indirect(entries(src_t, a, b)), COPY)
 
-        def finish_plainly(m, a, b, fetched):
+        def finish_plainly(m, fetched, gates, a, b):
             result = fresh("result_%d" % m, a, b)
-            nc.vector.tensor_tensor(result, fetched, gates[m][:, a:b], MULT)
+            nc.vector.tensor_tensor(result, fetched, gates[:, a:b], MULT)
             store(m, a, b, result)
 
-        second = [bank(5), bank(7)]
-        for number, (a, b) in enumerate(spans(PIECES)):
-            product(Y, 0, a, b, number, on_scalar)
-            if b % RUN == 0:
-                one_pass(second[a // BANK][:, (b - RUN) % BANK : (b - RUN) % BANK + RUN], Y, 1, b - RUN, b)
-        for half, (a, b) in enumerate(spans(HALVES)):
-            on_vector(out=tables[Y][1][:, a:b], in_=second[half][:])
-        product(E, 0, 0, BANK, 6, on_scalar)
-        product(E, 0, BANK, S, 0, on_vector)
-        product(E, 1, 0, BANK, 1, on_vector)
-        product(E, 1, BANK, S, 2, on_vector)
-        for m in blocks:
-            for a, b in spans(HALVES):
-                pick(m, a, b)
-                add(m, a, b)
-        product(H, 0, 0, BANK, 0, on_scalar)
-        product(H, 0, BANK, S, 1, on_scalar)
-        for a, b in spans(HALVES):
-            gate(0, a, b)
-            finish(0, a, b)
-        product(H, 1, 0, BANK, 2, on_scalar)
-        product(H, 1, BANK, S, 0, on_scalar)
-        parts = spans(LAST_CUTS)
-        for (a, b), (c, d) in zip(parts[0::2], parts[1::2]):
-            gate(1, a, d)
-            fetched = fetch(1, c, d)
-            finish(1, a, b)
-            finish_plainly(1, c, d, fetched)
-        a, b = parts[-1]
-        gate(1, a, b)
-        finish(1, a, b)
+        y0, y1, e0, e1, h0, h1 = (table(i, m) for i in (Y, E, H) for m in range(2))
+        riding = bank(2)
+        for q in range(2):
+            a, b = q * RUN, (q + 1) * RUN
+            on_scalar(out=y0[:, a:b], in_=product(Y, 0, a, b, q))
+            one_pass(riding[:, a:b], Y, 1, a, b)
+        on_vector(out=y1[:, 0:BANK], in_=riding[:])
+        on_scalar(out=e0[:, 0:BANK], in_=product(E, 0, 0, BANK, 3))
+        on_vector(out=h0[:, 0:BANK], in_=product(H, 0, 0, BANK, 4))
+        on_scalar(out=y0[:, BANK:S], in_=product(Y, 0, BANK, S, 5))
+        on_vector(out=h0[:, BANK:S], in_=product(H, 0, BANK, S, 6))
+        on_scalar(out=e0[:, BANK:S], in_=product(E, 0, BANK, S, 7))
+        on_vector(out=y1[:, BANK:S], in_=product(Y, 1, BANK, S, 0))
+        on_vector(out=e1[:, 0:BANK], in_=product(E, 1, 0, BANK, 1))
+        on_vector(out=h1[:, 0:BANK], in_=product(H, 1, 0, BANK, 2))
+        late_e = product(E, 1, BANK, S, 3)
+        late_h = product(H, 1, BANK, S, 4)
+
+        logits = [keep.tile([P, U], F32, name="logits_%d" % m) for m in range(2)]
+        gates = [keep.tile([P, U], F32, name="gates_%d" % m) for m in range(2)]
+        halves = spans((0, BANK, U))
+        picked = [h1[:, BANK:S], fresh("picked", BANK, U, tag="picked")]
+        for half, (a, b) in enumerate(halves):
+            pick(picked[half], y0, a, b)
+            add(logits[0][:, a:b], e0, picked[half], a, b)
+        on_scalar(out=e1[:, BANK:S], in_=late_e)
+        gate(gates[0][:, 0:BANK], logits[0][:, 0:BANK])
+        on_scalar(out=h1[:, BANK:S], in_=late_h)
+        gate(gates[0][:, BANK:U], logits[0][:, BANK:U])
+        for a, b in halves:
+            finish(0, h0, gates[0], a, b)
+        picked = keep.tile([P, U], F32, name="picked_1", tag="picked")
+        for a, b in halves:
+            pick(picked[:, a:b], y1, a, b)
+            add(logits[1][:, a:b], e1, picked[:, a:b], a, b)
+        first = fresh("fetched", 0, 256)
+        fetch(first, h1, 0, 256)
+        gate(gates[1][:, 0:BANK], logits[1][:, 0:BANK])
+        finish_plainly(1, first, gates[1], 0, 256)
+        finish(1, h1, gates[1], 256, 512)
+        fetch(picked[:, 0:256], h1, 512, 768)
+        gate(gates[1][:, 512:768], logits[1][:, 512:768])
+        finish_plainly(1, picked[:, 0:256], gates[1], 512, 768)
+        gate(gates[1][:, 768:U], logits[1][:, 768:U])
+        finish(1, h1, gates[1], 768, 896)
+        fetch(picked[:, 512:640], h1, 896, U)
+        finish_plainly(1, picked[:, 512:640], gates[1], 896, U)

@@ -95,6 +95,9 @@ def tile_picked_edgeatt_sigmoid_e_kernel(
 
         idle_codes = keep.tile([P, BANK // THIN, THIN], I32, name="idle_codes", align_bytes=64)
         nc.gpsimd.tensor_copy(out=idle_codes[:], in_=w_codes[Y][:, 0:THIN].unsqueeze(1).to_broadcast([P, BANK // THIN, THIN]))
+        idle_scales = keep.tile([P, BANK // THIN, THIN // 4], I32, name="idle_scales", align_bytes=64)
+        head = w_scales[:, 0:THIN].bitcast(I32)
+        nc.gpsimd.tensor_copy(out=idle_scales[:], in_=head.unsqueeze(1).to_broadcast([P, BANK // THIN, THIN // 4]))
         idle = psum.tile([P, BANK], F32, name="bank_7")
         for turn in range(4):
             nc.tensor.matmul_mx(
@@ -102,7 +105,7 @@ def tile_picked_edgeatt_sigmoid_e_kernel(
                 lhsT=w_codes[Y][:, 0:THIN].bitcast(FP8X4),
                 lhsT_scale=w_scales[:, 0:THIN],
                 rhs=idle_codes[:].rearrange("p a b -> p (a b)").bitcast(FP8X4),
-                rhs_scale=w_scales[:, 0:BANK],
+                rhs_scale=idle_scales[:].rearrange("p a b -> p (a b)").bitcast(U8),
                 start=True,
                 stop=True,
             )

@@ -25,7 +25,8 @@ Y, E, H = 0, 1, 2
 RUN = 256
 ORDER = (2, 0, 1, 3)
 EVEN = S // 2
-MID = (288, 704)
+MID = (288, 672)
+PIECES = (0, 256, 512, 896, S)
 THIN = 32
 
 
@@ -123,13 +124,13 @@ def tile_picked_edgeatt_sigmoid_e_kernel(
             else:
                 weave_vector(j, *MID)
                 weave_scalar(j, 0, MID[0])
-                for a, b in spans((MID[1], S - RUN, S) if j == ORDER[-1] else (MID[1], S)):
+                for a, b in spans((MID[1], PIECES[-2], S) if j == ORDER[-1] else (MID[1], S)):
                     weave_scalar(j, a, b)
-        for a in range(0, S, RUN):
+        for a, b in spans(PIECES):
             nc.vector.quantize_mx(
-                out=x_codes[:, a : a + RUN].bitcast(FP8X4),
-                scales=x_scales[:, a : a + RUN],
-                in_=woven[:, a : a + RUN, :].rearrange("p n j -> p (n j)"),
+                out=x_codes[:, a:b].bitcast(FP8X4),
+                scales=x_scales[:, a:b],
+                in_=woven[:, a:b, :].rearrange("p n j -> p (n j)"),
             )
 
         def table(i, m, tag=""):

@@ -81,12 +81,12 @@ def tile_picked_edgeatt_sigmoid_e_kernel(
 
         load_plane(0)
         nc.sync.dma_start(offs_t[:], offs)
-        load_codes(Y, 0, THIN)
         load_scales(E)
         load_plane(1)
         load_scales(H)
         load_plane(2)
         load_scales(Y)
+        load_codes(Y, 0, THIN)
         load_plane(3)
         load_codes(Y, THIN, N)
         load_codes(E, 0, N)

@@ -81,30 +81,30 @@ def tile_picked_edgeatt_sigmoid_e_kernel(
 
         load_plane(0)
         nc.sync.dma_start(offs_t[:], offs)
-        load_scales(E)
+        load_scales(Y)
         load_plane(1)
         load_scales(H)
         load_plane(2)
-        load_scales(Y)
-        load_codes(Y, 0, THIN)
+        load_scales(E)
+        load_codes(E, 0, THIN)
         load_plane(3)
-        load_codes(Y, THIN, N)
-        load_codes(E, 0, N)
+        load_codes(E, THIN, N)
+        load_codes(Y, 0, N)
         load_codes(H, 0, N)
-        nc.sync.dma_start(dst_t[:], dst)
         nc.sync.dma_start(src_t[:], src)
+        nc.sync.dma_start(dst_t[:], dst)
 
         idle_codes = keep.tile([P, BANK // THIN, THIN], I32, name="idle_codes", align_bytes=64)
-        nc.gpsimd.tensor_copy(out=idle_codes[:], in_=w_codes[Y][:, 0:THIN].unsqueeze(1).to_broadcast([P, BANK // THIN, THIN]))
+        nc.gpsimd.tensor_copy(out=idle_codes[:], in_=w_codes[E][:, 0:THIN].unsqueeze(1).to_broadcast([P, BANK // THIN, THIN]))
         idle_scales = keep.tile([P, BANK // THIN, THIN // 4], I32, name="idle_scales", align_bytes=64)
-        head = w_scales[:, 0:THIN].bitcast(I32)
+        head = w_scales[:, N : N + THIN].bitcast(I32)
         nc.gpsimd.tensor_copy(out=idle_scales[:], in_=head.unsqueeze(1).to_broadcast([P, BANK // THIN, THIN // 4]))
         idle = psum.tile([P, BANK], F32, name="bank_7")
         for turn in range(4):
             nc.tensor.matmul_mx(
                 out=idle[0:THIN, :],
-                lhsT=w_codes[Y][:, 0:THIN].bitcast(FP8X4),
-                lhsT_scale=w_scales[:, 0:THIN],
+                lhsT=w_codes[E][:, 0:THIN].bitcast(FP8X4),
+                lhsT_scale=w_scales[:, N : N + THIN],
                 rhs=idle_codes[:].rearrange("p a b -> p (a b)").bitcast(FP8X4),
                 rhs_scale=idle_scales[:].rearrange("p a b -> p (a b)").bitcast(U8),
                 start=True,
@@ -160,11 +160,11 @@ def tile_picked_edgeatt_sigmoid_e_kernel(
         def fresh(name, a, b, tag=""):
             return keep.tile([P, b - a], F32, name="%s_%d" % (name, a), tag=tag)[:]
 
-        def pick(target, y, a, b):
-            nc.scalar.activation(target, y[:].indirect(entries(dst_t, a, b)), COPY)
+        def pick(target, e, a, b):
+            nc.scalar.activation(target, e[:].indirect(entries(src_t, a, b)), COPY)
 
-        def add(target, e, picked, a, b):
-            nc.vector.tensor_tensor(target, e[:].indirect(entries(src_t, a, b)), picked, ADD)
+        def add(target, y, picked, a, b):
+            nc.vector.tensor_tensor(target, y[:].indirect(entries(dst_t, a, b)), picked, ADD)
 
         def gate(target, logits):
             nc.scalar.activation(target, logits, SIGMOID)
@@ -185,22 +185,22 @@ def tile_picked_edgeatt_sigmoid_e_kernel(
             nc.vector.tensor_tensor(result, fetched, gates[:, a:b], MULT)
             store(m, a, b, result)
 
-        y0, y1, e0, e1, h0, h1 = (table(i, m) for i in (Y, E, H) for m in range(2))
+        e0, e1, y0, y1, h0, h1 = (table(i, m) for i in (E, Y, H) for m in range(2))
         riding = bank(2)
         for q in range(2):
             a, b = q * RUN, (q + 1) * RUN
-            on_scalar(out=y0[:, a:b], in_=product(Y, 0, a, b, q))
-            one_pass(riding[:, a:b], Y, 1, a, b)
-        on_vector(out=y1[:, 0:BANK], in_=riding[:])
-        on_scalar(out=e0[:, 0:BANK], in_=product(E, 0, 0, BANK, 3))
+            on_scalar(out=e0[:, a:b], in_=product(E, 0, a, b, q))
+            one_pass(riding[:, a:b], E, 1, a, b)
+        on_vector(out=e1[:, 0:BANK], in_=riding[:])
+        on_scalar(out=y0[:, 0:BANK], in_=product(Y, 0, 0, BANK, 3))
         on_vector(out=h0[:, 0:BANK], in_=product(H, 0, 0, BANK, 4))
-        on_scalar(out=y0[:, BANK:S], in_=product(Y, 0, BANK, S, 5))
+        on_scalar(out=e0[:, BANK:S], in_=product(E, 0, BANK, S, 5))
         on_vector(out=h0[:, BANK:S], in_=product(H, 0, BANK, S, 6))
-        on_scalar(out=e0[:, BANK:S], in_=product(E, 0, BANK, S, 7))
-        on_vector(out=y1[:, BANK:S], in_=product(Y, 1, BANK, S, 0))
-        on_vector(out=e1[:, 0:BANK], in_=product(E, 1, 0, BANK, 1))
+        on_scalar(out=y0[:, BANK:S], in_=product(Y, 0, BANK, S, 7))
+        on_vector(out=e1[:, BANK:S], in_=product(E, 1, BANK, S, 0))
+        on_vector(out=y1[:, 0:BANK], in_=product(Y, 1, 0, BANK, 1))
         on_vector(out=h1[:, 0:BANK], in_=product(H, 1, 0, BANK, 2))
-        late_e = product(E, 1, BANK, S, 3)
+        late_y = product(Y, 1, BANK, S, 3)
         late_h = product(H, 1, BANK, S, 4)
 
         logits = [keep.tile([P, U], F32, name="logits_%d" % m) for m in range(2)]
@@ -208,9 +208,9 @@ def tile_picked_edgeatt_sigmoid_e_kernel(
         halves = spans((0, BANK, U))
         picked = [h1[:, BANK:S], fresh("picked", BANK, U, tag="picked")]
         for half, (a, b) in enumerate(halves):
-            pick(picked[half], y0, a, b)
-            add(logits[0][:, a:b], e0, picked[half], a, b)
-        on_scalar(out=e1[:, BANK:S], in_=late_e)
+            pick(picked[half], e0, a, b)
+            add(logits[0][:, a:b], y0, picked[half], a, b)
+        on_scalar(out=y1[:, BANK:S], in_=late_y)
         gate(gates[0][:, 0:BANK], logits[0][:, 0:BANK])
         on_scalar(out=h1[:, BANK:S], in_=late_h)
         gate(gates[0][:, BANK:U], logits[0][:, BANK:U])
@@ -218,8 +218,8 @@ def tile_picked_edgeatt_sigmoid_e_kernel(
             finish(0, h0, gates[0], a, b)
         picked = keep.tile([P, U], F32, name="picked_1", tag="picked")
         for a, b in halves:
-            pick(picked[:, a:b], y1, a, b)
-            add(logits[1][:, a:b], e1, picked[:, a:b], a, b)
+            pick(picked[:, a:b], e1, a, b)
+            add(logits[1][:, a:b], y1, picked[:, a:b], a, b)
         first = fresh("fetched", 0, 256)
         fetch(first, h1, 0, 256)
         gate(gates[1][:, 0:BANK], logits[1][:, 0:BANK])

from contextlib import ExitStack

import concourse.mybir as mybir

K, T, S, N, U = 512, 2048, 1024, 256, 1024
FLOPS = 3 * 2 * K * N * S

F32 = mybir.dt.float32
BF16 = mybir.dt.bfloat16
I32 = mybir.dt.int32
U32 = mybir.dt.uint32
U16 = mybir.dt.uint16
U8 = mybir.dt.uint8
FP8X4 = mybir.dt.float8_e4m3fn_x4
ADD = mybir.AluOpType.add
MULT = mybir.AluOpType.mult
COPY = mybir.ActivationFunctionType.Copy
SIGMOID = mybir.ActivationFunctionType.Sigmoid

P = 128
PACK = 4
BANK = 512
Y, E, H = 0, 1, 2

RUN = 256
ORDER = (2, 0, 1, 3)
EVEN = S // 2
MID = (288, 672)
PIECES = (0, 256, 512, 896, S)
THIN = 32


def entries(lst, a, b):
    return lst[:, a // 16 : b // 16]


def spans(cuts):
    return list(zip(cuts, cuts[1:]))


def tile_picked_edgeatt_sigmoid_e_kernel(
    tc, xT, w1_words, w1_scales, w2_words, w2_scales, w3_words, w3_scales, offs, src, dst, out
):
    nc = tc.nc
    with ExitStack() as ctx:
        keep = ctx.enter_context(tc.tile_pool(name="keep", bufs=1))
        psum = ctx.enter_context(tc.psum_pool(name="psum", bufs=1))

        offs_t = keep.tile([P, S // 16], U16, name="offs_t")
        src_t = keep.tile([P, U // 16], U16, name="src_t")
        dst_t = keep.tile([P, U // 16], U16, name="dst_t")
        x32 = [keep.tile([P, T], F32, name="x32_%d" % j) for j in range(PACK)]
        woven = keep.tile([P, S, PACK], BF16, name="woven", align_bytes=64)
        x_codes = keep.tile([P, S], U32, name="x_codes", align_bytes=64)
        x_scales = keep.tile([P, S], U8, name="x_scales", align_bytes=64)
        w_codes = [keep.tile([P, N], I32, name="w_codes_%d" % i, align_bytes=64) for i in (Y, E, H)]
        w_scales = keep.tile([P, 3 * N], U8, name="w_scales", align_bytes=64)
        words_in = (w1_words, w2_words, w3_words)
        scales_in = (w1_scales, w2_scales, w3_scales)

        nc.vector.memset(w_scales[:].bitcast(I32), 0)

        warm = keep.tile([P, 2], F32, name="warm")
        nc.vector.memset(warm[:, 0:1], 0.0)
        nc.scalar.activation(warm[:, 1:2], warm[:, 0:1], SIGMOID)

        def load_scales(i):
            rows = scales_in[i][0].bitcast(I32)
            for q in range(4):
                target = w_scales[32 * q : 32 * q + 4, i * N : (i + 1) * N]
                nc.sync.dma_start(out=target.bitcast(I32), in_=rows[4 * q : 4 * q + 4, :])

        def load_codes(i, a, b):
            words = words_in[i][0].rearrange("p n t -> p (n t)").bitcast(I32)
            nc.sync.dma_start(out=w_codes[i][:, a:b], in_=words[:, a:b])

        planes = xT.rearrange("(p j) t -> j p t", j=PACK)

        def load_plane(turn):
            nc.sync.dma_start(out=x32[ORDER[turn]][:], in_=planes[ORDER[turn]])

        load_plane(0)
        nc.sync.dma_start(offs_t[:], offs)
        load_scales(Y)
        load_plane(1)
        load_scales(H)
        load_plane(2)
        load_scales(E)
        load_codes(E, 0, THIN)
        load_plane(3)
        load_codes(E, THIN, N)
        load_codes(Y, 0, N)
        load_codes(H, 0, N)
        nc.sync.dma_start(src_t[:], src)
        nc.sync.dma_start(dst_t[:], dst)

        idle_codes = keep.tile([P, BANK // THIN, THIN], I32, name="idle_codes", align_bytes=64)
        nc.gpsimd.tensor_copy(out=idle_codes[:], in_=w_codes[E][:, 0:THIN].unsqueeze(1).to_broadcast([P, BANK // THIN, THIN]))
        idle_scales = keep.tile([P, BANK // THIN, THIN // 4], I32, name="idle_scales", align_bytes=64)
        head = w_scales[:, N : N + THIN].bitcast(I32)
        nc.gpsimd.tensor_copy(out=idle_scales[:], in_=head.unsqueeze(1).to_broadcast([P, BANK // THIN, THIN // 4]))
        idle = psum.tile([P, BANK], F32, name="bank_7")
        for turn in range(4):
            nc.tensor.matmul_mx(
                out=idle[0:THIN, :],
                lhsT=w_codes[E][:, 0:THIN].bitcast(FP8X4),
                lhsT_scale=w_scales[:, N : N + THIN],
                rhs=idle_codes[:].rearrange("p a b -> p (a b)").bitcast(FP8X4),
                rhs_scale=idle_scales[:].rearrange("p a b -> p (a b)").bitcast(U8),
                start=True,
                stop=True,
            )

        def weave_vector(j, a, b):
            nc.vector.tensor_copy(out=woven[:, a:b, j], in_=x32[j][:].indirect(entries(offs_t, a, b)))

        def weave_scalar(j, a, b):
            nc.scalar.activation(woven[:, a:b, j], x32[j][:].indirect(entries(offs_t, a, b)), COPY)

        for j in ORDER:
            if j < 2:
                weave_vector(j, 0, EVEN)
                weave_scalar(j, EVEN, S)
            else:
                weave_vector(j, *MID)
                weave_scalar(j, 0, MID[0])
                for a, b in spans((MID[1], PIECES[-2], S) if j == ORDER[-1] else (MID[1], S)):
                    weave_scalar(j, a, b)
        for a, b in spans(PIECES):
            nc.vector.quantize_mx(
                out=x_codes[:, a:b].bitcast(FP8X4),
                scales=x_scales[:, a:b],
                in_=woven[:, a:b, :].rearrange("p n j -> p (n j)"),
            )

        def table(i, m, tag=""):
            return keep.tile([P, S], F32, name="table_%d_%d" % (i, m), tag=tag)

        on_vector, on_scalar = nc.vector.tensor_copy, nc.scalar.copy

        def bank(number):
            return psum.tile([P, BANK], F32, name="bank_%d" % number)

        def one_pass(target, i, m, a, b):
            nc.tensor.matmul_mx(
                out=target,
                lhsT=w_codes[i][:, m * P : (m + 1) * P].bitcast(FP8X4),
                lhsT_scale=w_scales[:, i * N + m * P : i * N + (m + 1) * P],
                rhs=x_codes[:, a:b].bitcast(FP8X4),
                rhs_scale=x_scales[:, a:b],
                start=True,
                stop=True,
            )

        def product(i, m, a, b, number):
            target = bank(number)[:, 0 : b - a]
            one_pass(target, i, m, a, b)
            return target

        def fresh(name, a, b, tag=""):
            return keep.tile([P, b - a], F32, name="%s_%d" % (name, a), tag=tag)[:]

        def pick(target, e, a, b):
            nc.scalar.activation(target, e[:].indirect(entries(src_t, a, b)), COPY)

        def add(target, y, picked, a, b):
            nc.vector.tensor_tensor(target, y[:].indirect(entries(dst_t, a, b)), picked, ADD)

        def gate(target, logits):
            nc.scalar.activation(target, logits, SIGMOID)

        def store(m, a, b, result):
            nc.sync.dma_start(out=out[m * P : (m + 1) * P, a:b], in_=result)

        def finish(m, h, gates, a, b):
            result = fresh("result_%d" % m, a, b)
            nc.vector.tensor_tensor(result, h[:].indirect(entries(src_t, a, b)), gates[:, a:b], MULT)
            store(m, a, b, result)

        def fetch(target, h, a, b):
            nc.scalar.activation(target, h[:].indirect(entries(src_t, a, b)), COPY)

        def finish_plainly(m, fetched, gates, a, b):
            result = fresh("result_%d" % m, a, b)
            nc.vector.tensor_tensor(result, fetched, gates[:, a:b], MULT)
            store(m, a, b, result)

        e0, e1, y0, y1, h0, h1 = (table(i, m) for i in (E, Y, H) for m in range(2))
        riding = bank(2)
        for q in range(2):
            a, b = q * RUN, (q + 1) * RUN
            on_scalar(out=e0[:, a:b], in_=product(E, 0, a, b, q))
            one_pass(riding[:, a:b], E, 1, a, b)
        on_vector(out=e1[:, 0:BANK], in_=riding[:])
        on_scalar(out=y0[:, 0:BANK], in_=product(Y, 0, 0, BANK, 3))
        on_vector(out=h0[:, 0:BANK], in_=product(H, 0, 0, BANK, 4))
        on_scalar(out=e0[:, BANK:S], in_=product(E, 0, BANK, S, 5))
        on_vector(out=h0[:, BANK:S], in_=product(H, 0, BANK, S, 6))
        on_scalar(out=y0[:, BANK:S], in_=product(Y, 0, BANK, S, 7))
        on_vector(out=e1[:, BANK:S], in_=product(E, 1, BANK, S, 0))
        on_vector(out=y1[:, 0:BANK], in_=product(Y, 1, 0, BANK, 1))
        on_vector(out=h1[:, 0:BANK], in_=product(H, 1, 0, BANK, 2))
        late_y = product(Y, 1, BANK, S, 3)
        late_h = product(H, 1, BANK, S, 4)

        logits = [keep.tile([P, U], F32, name="logits_%d" % m) for m in range(2)]
        gates = [keep.tile([P, U], F32, name="gates_%d" % m) for m in range(2)]
        halves = spans((0, BANK, U))
        picked = [h1[:, BANK:S], fresh("picked", BANK, U, tag="picked")]
        for half, (a, b) in enumerate(halves):
            pick(picked[half], e0, a, b)
            add(logits[0][:, a:b], y0, picked[half], a, b)
        on_scalar(out=y1[:, BANK:S], in_=late_y)
        gate(gates[0][:, 0:BANK], logits[0][:, 0:BANK])
        on_scalar(out=h1[:, BANK:S], in_=late_h)
        gate(gates[0][:, BANK:U], logits[0][:, BANK:U])
        for a, b in halves:
            finish(0, h0, gates[0], a, b)
        picked = keep.tile([P, U], F32, name="picked_1", tag="picked")
        for a, b in halves:
            pick(picked[:, a:b], e1, a, b)
            add(logits[1][:, a:b], y1, picked[:, a:b], a, b)
        first = fresh("fetched", 0, 256)
        fetch(first, h1, 0, 256)
        gate(gates[1][:, 0:BANK], logits[1][:, 0:BANK])
        finish_plainly(1, first, gates[1], 0, 256)
        finish(1, h1, gates[1], 256, 512)
        fetch(picked[:, 0:256], h1, 512, 768)
        gate(gates[1][:, 512:768], logits[1][:, 512:768])
        finish_plainly(1, picked[:, 0:256], gates[1], 512, 768)
        gate(gates[1][:, 768:U], logits[1][:, 768:U])
        finish(1, h1, gates[1], 768, 896)
        fetch(picked[:, 512:640], h1, 896, U)
        finish_plainly(1, picked[:, 512:640], gates[1], 896, U)
